import numpy as np
import ml_dtypes


def mxq(x, axis, fmt="e4m3"):
    dtype, down = {"e4m3": (ml_dtypes.float8_e4m3fn, 7), "e5m2": (ml_dtypes.float8_e5m2, 14)}[fmt]
    v = np.moveaxis(np.asarray(x, np.float32).astype(ml_dtypes.bfloat16).astype(np.float64), axis, -1)
    blocks = v.reshape(v.shape[:-1] + (-1, 32))
    amax = np.abs(blocks).max(-1, keepdims=True)
    byte = np.maximum(np.where(amax > 0, np.frexp(amax)[1] - 1 + 127, 0) - down, 1)
    scale = np.exp2(byte - 127.0)
    codes = (blocks / scale).astype(np.float32).astype(dtype).astype(np.float64)
    return np.moveaxis((codes * scale).reshape(v.shape), -1, axis)


WIDE = False


def mx_kscale(k):
    if not WIDE:
        return np.ones(k)
    levels = np.array([10, -10, 5, -5, 0])
    if k % 512:
        return np.exp2(np.random.permutation(np.resize(levels, k // 32))).repeat(32)
    a = np.empty((k // 512, 16))
    for p in range(k // 512):
        a[p, :8] = np.random.permutation(np.resize(levels, 8))
        for g in range(8):
            far = levels[np.abs(levels - a[p, g]) >= 10]
            a[p, g + 8] = far[np.random.randint(len(far))]
    return np.exp2(a.ravel()).repeat(32)


def f64(x):
    return np.asarray(x).astype(np.float64)


def striped(idx):
    return np.tile(idx.reshape(-1, 16).T, (8, 1)).astype(np.uint16)


def unstriped(offs):
    return offs[:16].T.reshape(-1).astype(np.int64)


def pack_weight(w):
    k, n = w.shape
    w = f64(np.asarray(w, np.float32).astype(ml_dtypes.bfloat16)).reshape(k // 32, 32, n)
    amax = np.abs(w).max(1)
    byte = np.clip(np.where(amax > 0, np.frexp(amax)[1] - 1 + 127 - 7, 1), 1, 254)
    scaled = (w * np.exp2(127.0 - byte)[:, None, :]).reshape(k, n).astype(np.float32)
    words = np.ascontiguousarray(scaled.reshape(k // 512, 128, 4, n).transpose(0, 1, 3, 2)).astype(ml_dtypes.float8_e4m3fn).view(np.uint8)
    return words, np.ascontiguousarray(byte.astype(np.uint8).reshape(k // 512, 16, n))


def unpack_weight(words, scales):
    g, p, n, _ = words.shape
    vals = np.ascontiguousarray(words).view(ml_dtypes.float8_e4m3fn).astype(np.float64) * np.repeat(np.exp2(scales.astype(np.float64) - 127.0), 8, axis=1)[..., None]
    return vals.transpose(0, 1, 3, 2).reshape(g * 512, n)


K, T, S, V, N = 512, 1024, 512, 256, 128
P = 2 ** 7


def setup_inputs():
    n = np.random.standard_normal
    s = mx_kscale(K)[:, None]
    packed_w1 = pack_weight(n((K, N)) / np.sqrt(K) / s)
    return {
        "xT": (n((K, T)) * s).astype(np.float32),
        "w1_words": packed_w1[0],
        "w1_scales": packed_w1[1],
        "bound": np.tile(np.random.uniform(0.3, 1.2, V), (P, 1)).astype(np.float32),
        "offs": striped(np.random.permutation(T)[:S]),
        "cen": striped(np.random.permutation(S)[:V]),
        "pos1": striped(np.random.permutation(S)[:V]),
        "pos2": striped(np.random.permutation(S)[:V]),
        "pos3": striped(np.random.permutation(S)[:V]),
        "pos4": striped(np.random.permutation(S)[:V]),
    }


def reference(xT, w1_words, w1_scales, bound, offs, cen, pos1, pos2, pos3, pos4):
    xq = mxq(f64(xT)[:, unstriped(offs)], 0, "e4m3")
    y = unpack_weight(w1_words, w1_scales).T @ xq
    yc = y[:, unstriped(cen)]
    low = -1.0 * f64(bound)[:1]
    return yc + (np.maximum(np.minimum(y[:, unstriped(pos1)] - yc, f64(bound)[:1]), low) + np.maximum(np.minimum(y[:, unstriped(pos2)] - yc, f64(bound)[:1]), low) + np.maximum(np.minimum(y[:, unstriped(pos3)] - yc, f64(bound)[:1]), low) + np.maximum(np.minimum(y[:, unstriped(pos4)] - yc, f64(bound)[:1]), low)) / 4

@@ -1,0 +1,150 @@
+from contextlib import ExitStack
+
+import concourse.mybir as mybir
+from concourse.masks import make_identity
+
+K, T, S, V, N = 512, 1024, 512, 256, 128
+D = 4
+FLOPS = 2 * K * N * S
+
+F32 = mybir.dt.float32
+BF16 = mybir.dt.bfloat16
+I32 = mybir.dt.int32
+U32 = mybir.dt.uint32
+U16 = mybir.dt.uint16
+U8 = mybir.dt.uint8
+FP8X4 = mybir.dt.float8_e4m3fn_x4
+ALU = mybir.AluOpType
+
+P = 128
+PACK = 4
+PIECE = 128
+PIECES = S // PIECE
+HALVES = V // P
+LANE = 16
+
+
+def entries(offsets, first, count):
+    return offsets[:, first // LANE : (first + count) // LANE]
+
+
+def tile_picked_huber_none_e_kernel(
+    tc, xT, w1_words, w1_scales, bound, offs, cen, pos1, pos2, pos3, pos4, out
+):
+    nc = tc.nc
+    with ExitStack() as ctx:
+        keep = ctx.enter_context(tc.tile_pool(name="keep", bufs=1))
+        psum = ctx.enter_context(tc.psum_pool(name="psum", bufs=1))
+
+        def bank(i, width):
+            return psum.tile([P, width], F32, name=f"bank{i}", tag=f"bank{i}")
+
+        rows = xT.rearrange("(p j) t -> j p t", j=PACK)
+        planes = [keep.tile([P, T], F32, name=f"plane{j}") for j in range(PACK)]
+        picked = keep.tile([P, S // LANE], U16, name="picked")
+        nc.sync.dma_start(planes[0][:], rows[0])
+        nc.sync.dma_start(picked[:], offs)
+        for j in range(1, PACK):
+            nc.sync.dma_start(planes[j][:], rows[j])
+        w_codes = keep.tile([P, N], U32, name="w_codes", align_bytes=64)
+        nc.sync.dma_start(w_codes[:].bitcast(I32), w1_words[0].rearrange("p n t -> p (n t)").bitcast(I32))
+        centre = keep.tile([P, V // LANE], U16, name="centre")
+        nc.sync.dma_start(centre[:], cen)
+        near = []
+        for d, pos in enumerate((pos1, pos2, pos3, pos4)):
+            lst = keep.tile([P, V // LANE], U16, name=f"near{d}")
+            nc.sync.dma_start(lst[:], pos)
+            near.append(lst)
+        upper = keep.tile([P, HALVES], F32, name="upper")
+        with nc.allow_non_contiguous_dma(reason="one bound for each partition"):
+            nc.sync.dma_start(upper[:], bound[0:1, :].rearrange("o (h p) -> p (o h)", p=P))
+
+        ident = keep.tile([P, P], F32, name="ident")
+        make_identity(nc, ident[:])
+        w_scales = keep.tile([P, N], U8, name="w_scales", align_bytes=64)
+        nc.vector.memset(w_scales[:].bitcast(I32), 0)
+        for q in range(4):
+            nc.gpsimd.dma_start(
+                w_scales[32 * q : 32 * q + 4, :].bitcast(I32), w1_scales[0, 4 * q : 4 * q + 4, :].bitcast(I32)
+            )
+        lower = keep.tile([P, HALVES], F32, name="lower")
+        nc.gpsimd.tensor_scalar(lower[:], upper[:], -1.0, 0.0, ALU.mult, ALU.add)
+
+        grouped = [keep.tile([P, PIECE, PACK], BF16, name=f"grouped{c}", align_bytes=64) for c in range(PIECES)]
+        front = keep.tile([P, 2, 2, 2 * PIECE], BF16, name="front")
+        back = keep.tile([P, PIECES, 2, PIECE], BF16, name="back")
+        nc.vector.tensor_copy(front[:, :, 0, :], planes[0][:].indirect(picked[:]))
+        for u in range(2):
+            nc.vector.tensor_copy(front[:, u, 1, :], planes[1][:].indirect(entries(picked, 2 * PIECE * u, 2 * PIECE)))
+        for c in range(PIECES):
+            cols = slice((c % 2) * PIECE, (c % 2 + 1) * PIECE)
+            nc.scalar.copy(grouped[c][:, :, 0:2], front[:, c // 2, :, cols].rearrange("p j s -> p s j"))
+        nc.vector.tensor_copy(back[:, :, 0, :], planes[2][:].indirect(picked[:]))
+        for c in range(PIECES):
+            nc.vector.tensor_copy(back[:, c, 1, :], planes[3][:].indirect(entries(picked, PIECE * c, PIECE)))
+        for c in range(PIECES - 1):
+            nc.scalar.copy(grouped[c][:, :, 2:4], back[:, c].rearrange("p j s -> p s j"))
+
+        y = keep.tile([P, S], F32, name="y")
+
+        def project(c):
+            codes = keep.tile([P, PIECE], U32, name=f"codes{c}", align_bytes=64)
+            scales = keep.tile([P, PIECE], U8, name=f"scales{c}", align_bytes=64)
+            nc.vector.quantize_mx(
+                out=codes[:].bitcast(FP8X4), scales=scales[:], in_=grouped[c][:].rearrange("p s j -> p (s j)")
+            )
+            acc = bank(c, PIECE)
+            nc.tensor.matmul_mx(
+                out=acc[:], lhsT=w_codes[:].bitcast(FP8X4), lhsT_scale=w_scales[:],
+                rhs=codes[:].bitcast(FP8X4), rhs_scale=scales[:], start=True, stop=True,
+            )
+            nc.scalar.copy(y[:, c * PIECE : (c + 1) * PIECE], acc[:])
+
+        last = PIECES - 1
+        project(0)
+        nc.vector.tensor_copy(grouped[last][:, :, 2:4], back[:, last].rearrange("p j s -> p s j"))
+        project(1)
+        project(last)
+        project(2)
+
+        yc = [keep.tile([P, P], F32, name=f"yc{h}") for h in range(HALVES)]
+        for h in range(HALVES):
+            nc.vector.tensor_copy(yc[h][:], y[:].indirect(entries(centre, h * P, P)))
+
+        def pull(d, h, dest):
+            diff = keep.tile([P, P], F32, name=f"diff{d}_{h}")
+            nc.vector.tensor_tensor(diff[:], y[:].indirect(entries(near[d], h * P, P)), yc[h][:], ALU.subtract)
+            nc.tensor.transpose(dest, diff[:], ident[:])
+
+        def clip(h, turned, first, count, total):
+            clipped = keep.tile([P, count * P], F32, name=f"clipped{h}_{first}")
+            nc.vector.tensor_scalar(clipped[:], turned, upper[:, h : h + 1], lower[:, h : h + 1], ALU.min, ALU.max)
+            for i in range(count):
+                d = first + i
+                nc.tensor.matmul(
+                    total, lhsT=clipped[:, i * P : (i + 1) * P], rhs=ident[:],
+                    start=(d == 0), stop=(d == D - 1), is_transpose=True,
+                )
+
+        def finish(h, total):
+            res = keep.tile([P, P], F32, name=f"res{h}")
+            nc.vector.scalar_tensor_tensor(res[:], total, 1.0 / D, yc[h][:], ALU.mult, ALU.add)
+            nc.sync.dma_start(out[:, h * P : (h + 1) * P], res[:])
+
+        totals = [bank(4 + h, P) for h in range(HALVES)]
+        turned0 = bank(6, D * P)
+        turned1 = bank(7, 2 * P)
+        turned2 = bank(0, P)
+        turned3 = bank(1, P)
+        for d in range(D):
+            pull(d, 0, turned0[:, d * P : (d + 1) * P])
+        for d in range(2):
+            pull(d, 1, turned1[:, d * P : (d + 1) * P])
+        clip(0, turned0[:], 0, D, totals[0][:])
+        pull(2, 1, turned2[:])
+        pull(3, 1, turned3[:])
+        clip(1, turned1[:], 0, 2, totals[1][:])
+        clip(1, turned2[:], 2, 1, totals[1][:])
+        clip(1, turned3[:], 3, 1, totals[1][:])
+        finish(0, totals[0][:])
+        finish(1, totals[1][:])

@@ -15,6 +15,7 @@ U16 = mybir.dt.uint16
 U8 = mybir.dt.uint8
 FP8X4 = mybir.dt.float8_e4m3fn_x4
 ALU = mybir.AluOpType
+COPY = mybir.ActivationFunctionType.Copy
 
 P = 128
 PACK = 4
@@ -22,6 +23,7 @@ PIECE = 128
 PIECES = S // PIECE
 HALVES = V // P
 LANE = 16
+CAST_SPLIT = 256
 
 
 def entries(offsets, first, count):
@@ -39,6 +41,7 @@ def tile_picked_huber_none_e_kernel(
         def bank(i, width):
             return psum.tile([P, width], F32, name=f"bank{i}", tag=f"bank{i}")
 
+        w_scales = keep.tile([P, N], U8, name="w_scales", align_bytes=64)
         rows = xT.rearrange("(p j) t -> j p t", j=PACK)
         planes = [keep.tile([P, T], F32, name=f"plane{j}") for j in range(PACK)]
         picked = keep.tile([P, S // LANE], U16, name="picked")
@@ -48,6 +51,10 @@ def tile_picked_huber_none_e_kernel(
             nc.sync.dma_start(planes[j][:], rows[j])
         w_codes = keep.tile([P, N], U32, name="w_codes", align_bytes=64)
         nc.sync.dma_start(w_codes[:].bitcast(I32), w1_words[0].rearrange("p n t -> p (n t)").bitcast(I32))
+        for q in range(4):
+            nc.sync.dma_start(
+                w_scales[32 * q : 32 * q + 4, :].bitcast(I32), w1_scales[0, 4 * q : 4 * q + 4, :].bitcast(I32)
+            )
         centre = keep.tile([P, V // LANE], U16, name="centre")
         nc.sync.dma_start(centre[:], cen)
         near = []
@@ -61,24 +68,26 @@ def tile_picked_huber_none_e_kernel(
 
         ident = keep.tile([P, P], F32, name="ident")
         make_identity(nc, ident[:])
-        w_scales = keep.tile([P, N], U8, name="w_scales", align_bytes=64)
-        nc.vector.memset(w_scales[:].bitcast(I32), 0)
-        for q in range(4):
-            nc.gpsimd.dma_start(
-                w_scales[32 * q : 32 * q + 4, :].bitcast(I32), w1_scales[0, 4 * q : 4 * q + 4, :].bitcast(I32)
-            )
         lower = keep.tile([P, HALVES], F32, name="lower")
         nc.gpsimd.tensor_scalar(lower[:], upper[:], -1.0, 0.0, ALU.mult, ALU.add)
 
         grouped = [keep.tile([P, PIECE, PACK], BF16, name=f"grouped{c}", align_bytes=64) for c in range(PIECES)]
-        front = keep.tile([P, 2, 2, 2 * PIECE], BF16, name="front")
+        half = S // 2
+        front = keep.tile([P, 2, half], BF16, name="front")
+        second = keep.tile([P, half], BF16, name="second")
         back = keep.tile([P, PIECES, 2, PIECE], BF16, name="back")
-        nc.vector.tensor_copy(front[:, :, 0, :], planes[0][:].indirect(picked[:]))
-        for u in range(2):
-            nc.vector.tensor_copy(front[:, u, 1, :], planes[1][:].indirect(entries(picked, 2 * PIECE * u, 2 * PIECE)))
-        for c in range(PIECES):
-            cols = slice((c % 2) * PIECE, (c % 2 + 1) * PIECE)
-            nc.scalar.copy(grouped[c][:, :, 0:2], front[:, c // 2, :, cols].rearrange("p j s -> p s j"))
+        rounded = keep.tile([P, T], BF16, name="rounded")
+        nc.scalar.copy(rounded[:, 0:CAST_SPLIT], planes[0][:, 0:CAST_SPLIT])
+        nc.vector.tensor_copy(rounded[:, CAST_SPLIT:T], planes[0][:, CAST_SPLIT:T])
+        nc.vector.tensor_copy(front[:, 0, :], planes[0][:].indirect(entries(picked, 0, half)))
+        for c in range(2, PIECES):
+            nc.scalar.activation(grouped[c][:, :, 0], rounded[:].indirect(entries(picked, PIECE * c, PIECE)), COPY)
+        nc.vector.tensor_copy(front[:, 1, :], planes[1][:].indirect(entries(picked, 0, half)))
+        nc.vector.tensor_copy(second[:], planes[1][:].indirect(entries(picked, half, half)))
+        for c in range(2):
+            nc.scalar.copy(grouped[c][:, :, 0:2], front[:, :, c * PIECE : (c + 1) * PIECE].rearrange("p j s -> p s j"))
+        for c in range(2, PIECES):
+            nc.scalar.copy(grouped[c][:, :, 1], second[:, (c - 2) * PIECE : (c - 1) * PIECE])
         nc.vector.tensor_copy(back[:, :, 0, :], planes[2][:].indirect(picked[:]))
         for c in range(PIECES):
             nc.vector.tensor_copy(back[:, c, 1, :], planes[3][:].indirect(entries(picked, PIECE * c, PIECE)))
@@ -107,44 +116,45 @@ def tile_picked_huber_none_e_kernel(
         project(last)
         project(2)
 
-        yc = [keep.tile([P, P], F32, name=f"yc{h}") for h in range(HALVES)]
+        halves = [slice(h * P, (h + 1) * P) for h in range(HALVES)]
+        yc = keep.tile([P, V], F32, name="yc")
         for h in range(HALVES):
-            nc.vector.tensor_copy(yc[h][:], y[:].indirect(entries(centre, h * P, P)))
+            nc.vector.tensor_copy(yc[:, halves[h]], y[:].indirect(entries(centre, h * P, P)))
 
-        def pull(d, h, dest):
-            diff = keep.tile([P, P], F32, name=f"diff{d}_{h}")
-            nc.vector.tensor_tensor(diff[:], y[:].indirect(entries(near[d], h * P, P)), yc[h][:], ALU.subtract)
-            nc.tensor.transpose(dest, diff[:], ident[:])
+        early = [bank(6 + h, (D - 1) * P) for h in range(HALVES)]
+        late = [bank(h, P) for h in range(HALVES)]
+        totals = [bank(4 + h, P) for h in range(HALVES)]
 
-        def clip(h, turned, first, count, total):
+        def pull(d, first, count):
+            diff = keep.tile([P, count * P], F32, name=f"diff{d}_{first}")
+            cols = slice(first * P, (first + count) * P)
+            nc.vector.tensor_tensor(diff[:], y[:].indirect(entries(near[d], first * P, count * P)), yc[:, cols], ALU.subtract)
+            for i in range(count):
+                h = first + i
+                dest = late[h][:] if d == D - 1 else early[h][:, d * P : (d + 1) * P]
+                nc.tensor.transpose(dest, diff[:, i * P : (i + 1) * P], ident[:])
+
+        def clip(h, turned, first, count):
             clipped = keep.tile([P, count * P], F32, name=f"clipped{h}_{first}")
             nc.vector.tensor_scalar(clipped[:], turned, upper[:, h : h + 1], lower[:, h : h + 1], ALU.min, ALU.max)
             for i in range(count):
                 d = first + i
                 nc.tensor.matmul(
-                    total, lhsT=clipped[:, i * P : (i + 1) * P], rhs=ident[:],
+                    totals[h][:], lhsT=clipped[:, i * P : (i + 1) * P], rhs=ident[:],
                     start=(d == 0), stop=(d == D - 1), is_transpose=True,
                 )
 
-        def finish(h, total):
+        pull(0, 0, 1)
+        pull(0, 1, 1)
+        pull(1, 0, 2)
+        pull(2, 0, 2)
+        pull(3, 0, 1)
+        pull(3, 1, 1)
+        for h in range(HALVES):
+            clip(h, early[h][:], 0, D - 1)
+        for h in range(HALVES):
+            clip(h, late[h][:], D - 1, 1)
+        for h in range(HALVES):
             res = keep.tile([P, P], F32, name=f"res{h}")
-            nc.vector.scalar_tensor_tensor(res[:], total, 1.0 / D, yc[h][:], ALU.mult, ALU.add)
-            nc.sync.dma_start(out[:, h * P : (h + 1) * P], res[:])
-
-        totals = [bank(4 + h, P) for h in range(HALVES)]
-        turned0 = bank(6, D * P)
-        turned1 = bank(7, 2 * P)
-        turned2 = bank(0, P)
-        turned3 = bank(1, P)
-        for d in range(D):
-            pull(d, 0, turned0[:, d * P : (d + 1) * P])
-        for d in range(2):
-            pull(d, 1, turned1[:, d * P : (d + 1) * P])
-        clip(0, turned0[:], 0, D, totals[0][:])
-        pull(2, 1, turned2[:])
-        pull(3, 1, turned3[:])
-        clip(1, turned1[:], 0, 2, totals[1][:])
-        clip(1, turned2[:], 2, 1, totals[1][:])
-        clip(1, turned3[:], 3, 1, totals[1][:])
-        finish(0, totals[0][:])
-        finish(1, totals[1][:])
+            nc.vector.scalar_tensor_tensor(res[:], totals[h][:], 1.0 / D, yc[:, halves[h]], ALU.mult, ALU.add)
+            nc.sync.dma_start(out[:, halves[h]], res[:])

@@ -57,21 +57,19 @@ def tile_picked_huber_none_e_kernel(
             )
         centre = keep.tile([P, V // LANE], U16, name="centre")
         nc.sync.dma_start(centre[:], cen)
+        upper = keep.tile([P, HALVES], F32, name="upper")
+        with nc.allow_non_contiguous_dma(reason="one bound for each partition"):
+            nc.sync.dma_start(upper[:], bound[0:1, :].rearrange("o (h p) -> p (o h)", p=P))
         near = []
         for d, pos in enumerate((pos1, pos2, pos3, pos4)):
             lst = keep.tile([P, V // LANE], U16, name=f"near{d}")
             nc.sync.dma_start(lst[:], pos)
             near.append(lst)
-        upper = keep.tile([P, HALVES], F32, name="upper")
-        with nc.allow_non_contiguous_dma(reason="one bound for each partition"):
-            nc.sync.dma_start(upper[:], bound[0:1, :].rearrange("o (h p) -> p (o h)", p=P))
 
         ident = keep.tile([P, P], F32, name="ident")
         make_identity(nc, ident[:])
-        lower = keep.tile([P, HALVES], F32, name="lower")
-        nc.gpsimd.tensor_scalar(lower[:], upper[:], -1.0, 0.0, ALU.mult, ALU.add)
 
-        grouped = [keep.tile([P, PIECE, PACK], BF16, name=f"grouped{c}", align_bytes=64) for c in range(PIECES)]
+        grouped = [keep.tile([P, PIECE, PACK], BF16, name=f"grouped{c}", tag=f"grouped{c}", align_bytes=64) for c in range(PIECES)]
         half = S // 2
         front = keep.tile([P, 2, half], BF16, name="front")
         second = keep.tile([P, half], BF16, name="second")
@@ -89,10 +87,16 @@ def tile_picked_huber_none_e_kernel(
         for c in range(2, PIECES):
             nc.scalar.copy(grouped[c][:, :, 1], second[:, (c - 2) * PIECE : (c - 1) * PIECE])
         nc.vector.tensor_copy(back[:, :, 0, :], planes[2][:].indirect(picked[:]))
-        for c in range(PIECES):
-            nc.vector.tensor_copy(back[:, c, 1, :], planes[3][:].indirect(entries(picked, PIECE * c, PIECE)))
-        for c in range(PIECES - 1):
-            nc.scalar.copy(grouped[c][:, :, 2:4], back[:, c].rearrange("p j s -> p s j"))
+        runs = [(0, 0, PIECE // 2), (0, PIECE // 2, PIECE // 2)] + [(c, 0, PIECE) for c in range(1, PIECES)]
+        for c, first, count in runs:
+            nc.vector.tensor_copy(
+                back[:, c, 1, first : first + count], planes[3][:].indirect(entries(picked, PIECE * c + first, count))
+            )
+        for c, first, count in runs[:-1]:
+            nc.scalar.copy(
+                grouped[c][:, first : first + count, 2:4],
+                back[:, c, :, first : first + count].rearrange("p j s -> p s j"),
+            )
 
         y = keep.tile([P, S], F32, name="y")
 
@@ -107,7 +111,10 @@ def tile_picked_huber_none_e_kernel(
                 out=acc[:], lhsT=w_codes[:].bitcast(FP8X4), lhsT_scale=w_scales[:],
                 rhs=codes[:].bitcast(FP8X4), rhs_scale=scales[:], start=True, stop=True,
             )
-            nc.scalar.copy(y[:, c * PIECE : (c + 1) * PIECE], acc[:])
+            if c == 2:
+                nc.vector.tensor_copy(y[:, c * PIECE : (c + 1) * PIECE], acc[:])
+            else:
+                nc.scalar.copy(y[:, c * PIECE : (c + 1) * PIECE], acc[:])
 
         last = PIECES - 1
         project(0)
@@ -117,12 +124,17 @@ def tile_picked_huber_none_e_kernel(
         project(2)
 
         halves = [slice(h * P, (h + 1) * P) for h in range(HALVES)]
+        lower = keep.tile([P, HALVES], F32, name="lower", tag="grouped2", align_bytes=64)
+        nc.vector.tensor_scalar(lower[:], upper[:], -1.0, None, ALU.mult)
         yc = keep.tile([P, V], F32, name="yc")
         for h in range(HALVES):
             nc.vector.tensor_copy(yc[:, halves[h]], y[:].indirect(entries(centre, h * P, P)))
 
-        early = [bank(6 + h, (D - 1) * P) for h in range(HALVES)]
-        late = [bank(h, P) for h in range(HALVES)]
+        early = [bank(6 + h, 2 * P) for h in range(HALVES)]
+        turned = {(d, h): early[h][:, d * P : (d + 1) * P] for d in range(2) for h in range(HALVES)}
+        for d in range(2, D):
+            for h in range(HALVES):
+                turned[(d, h)] = bank(2 * (d - 2) + h, P)[:]
         totals = [bank(4 + h, P) for h in range(HALVES)]
 
         def pull(d, first, count):
@@ -131,12 +143,11 @@ def tile_picked_huber_none_e_kernel(
             nc.vector.tensor_tensor(diff[:], y[:].indirect(entries(near[d], first * P, count * P)), yc[:, cols], ALU.subtract)
             for i in range(count):
                 h = first + i
-                dest = late[h][:] if d == D - 1 else early[h][:, d * P : (d + 1) * P]
-                nc.tensor.transpose(dest, diff[:, i * P : (i + 1) * P], ident[:])
+                nc.tensor.transpose(turned[(d, h)], diff[:, i * P : (i + 1) * P], ident[:])
 
-        def clip(h, turned, first, count):
+        def clip(h, source, first, count):
             clipped = keep.tile([P, count * P], F32, name=f"clipped{h}_{first}")
-            nc.vector.tensor_scalar(clipped[:], turned, upper[:, h : h + 1], lower[:, h : h + 1], ALU.min, ALU.max)
+            nc.vector.tensor_scalar(clipped[:], source, upper[:, h : h + 1], lower[:, h : h + 1], ALU.min, ALU.max)
             for i in range(count):
                 d = first + i
                 nc.tensor.matmul(
@@ -150,10 +161,9 @@ def tile_picked_huber_none_e_kernel(
         pull(2, 0, 2)
         pull(3, 0, 1)
         pull(3, 1, 1)
-        for h in range(HALVES):
-            clip(h, early[h][:], 0, D - 1)
-        for h in range(HALVES):
-            clip(h, late[h][:], D - 1, 1)
+        for d in range(D):
+            for h in range(HALVES):
+                clip(h, turned[(d, h)], d, 1)
         for h in range(HALVES):
             res = keep.tile([P, P], F32, name=f"res{h}")
             nc.vector.scalar_tensor_tensor(res[:], totals[h][:], 1.0 / D, yc[:, halves[h]], ALU.mult, ALU.add)

@@ -72,20 +72,16 @@ def tile_picked_huber_none_e_kernel(
         grouped = [keep.tile([P, PIECE, PACK], BF16, name=f"grouped{c}", tag=f"grouped{c}", align_bytes=64) for c in range(PIECES)]
         half = S // 2
         front = keep.tile([P, 2, half], BF16, name="front")
-        second = keep.tile([P, half], BF16, name="second")
         back = keep.tile([P, PIECES, 2, PIECE], BF16, name="back")
-        rounded = keep.tile([P, T], BF16, name="rounded")
-        nc.scalar.copy(rounded[:, 0:CAST_SPLIT], planes[0][:, 0:CAST_SPLIT])
-        nc.vector.tensor_copy(rounded[:, CAST_SPLIT:T], planes[0][:, CAST_SPLIT:T])
-        nc.vector.tensor_copy(front[:, 0, :], planes[0][:].indirect(entries(picked, 0, half)))
-        for c in range(2, PIECES):
-            nc.scalar.activation(grouped[c][:, :, 0], rounded[:].indirect(entries(picked, PIECE * c, PIECE)), COPY)
-        nc.vector.tensor_copy(front[:, 1, :], planes[1][:].indirect(entries(picked, 0, half)))
-        nc.vector.tensor_copy(second[:], planes[1][:].indirect(entries(picked, half, half)))
+        for j in range(2):
+            rounded = keep.tile([P, T], BF16, name=f"rounded{j}")
+            nc.scalar.copy(rounded[:, 0:CAST_SPLIT], planes[j][:, 0:CAST_SPLIT])
+            nc.vector.tensor_copy(rounded[:, CAST_SPLIT:T], planes[j][:, CAST_SPLIT:T])
+            nc.vector.tensor_copy(front[:, j, :], planes[j][:].indirect(entries(picked, 0, half)))
+            for c in range(2, PIECES):
+                nc.scalar.activation(grouped[c][:, :, j], rounded[:].indirect(entries(picked, PIECE * c, PIECE)), COPY)
         for c in range(2):
             nc.scalar.copy(grouped[c][:, :, 0:2], front[:, :, c * PIECE : (c + 1) * PIECE].rearrange("p j s -> p s j"))
-        for c in range(2, PIECES):
-            nc.scalar.copy(grouped[c][:, :, 1], second[:, (c - 2) * PIECE : (c - 1) * PIECE])
         nc.vector.tensor_copy(back[:, :, 0, :], planes[2][:].indirect(picked[:]))
         runs = [(0, 0, PIECE // 2), (0, PIECE // 2, PIECE // 2)] + [(c, 0, PIECE) for c in range(1, PIECES)]
         for c, first, count in runs:

@@ -16,6 +16,8 @@ U8 = mybir.dt.uint8
 FP8X4 = mybir.dt.float8_e4m3fn_x4
 ALU = mybir.AluOpType
 COPY = mybir.ActivationFunctionType.Copy
+RELU = mybir.ActivationFunctionType.Relu
+IDENTITY = mybir.ActivationFunctionType.Identity
 
 P = 128
 PACK = 4
@@ -23,6 +25,7 @@ PIECE = 128
 PIECES = S // PIECE
 HALVES = V // P
 LANE = 16
+TURNED = 2
 CAST_SPLIT = 256
 
 
@@ -49,17 +52,19 @@ def tile_picked_huber_none_e_kernel(
         nc.sync.dma_start(picked[:], offs)
         for j in range(1, PACK):
             nc.sync.dma_start(planes[j][:], rows[j])
+        reach = keep.tile([P, V], F32, name="reach")
+        nc.sync.dma_start(reach[:], bound)
+        centre = keep.tile([P, V // LANE], U16, name="centre")
+        nc.sync.dma_start(centre[:], cen)
         w_codes = keep.tile([P, N], U32, name="w_codes", align_bytes=64)
         nc.sync.dma_start(w_codes[:].bitcast(I32), w1_words[0].rearrange("p n t -> p (n t)").bitcast(I32))
         for q in range(4):
             nc.sync.dma_start(
                 w_scales[32 * q : 32 * q + 4, :].bitcast(I32), w1_scales[0, 4 * q : 4 * q + 4, :].bitcast(I32)
             )
-        centre = keep.tile([P, V // LANE], U16, name="centre")
-        nc.sync.dma_start(centre[:], cen)
-        upper = keep.tile([P, HALVES], F32, name="upper")
+        reach_t = keep.tile([P, HALVES], F32, name="reach_t")
         with nc.allow_non_contiguous_dma(reason="one bound for each partition"):
-            nc.sync.dma_start(upper[:], bound[0:1, :].rearrange("o (h p) -> p (o h)", p=P))
+            nc.sync.dma_start(reach_t[:], bound[0:1, :].rearrange("o (h p) -> p (o h)", p=P))
         near = []
         for d, pos in enumerate((pos1, pos2, pos3, pos4)):
             lst = keep.tile([P, V // LANE], U16, name=f"near{d}")
@@ -68,11 +73,14 @@ def tile_picked_huber_none_e_kernel(
 
         ident = keep.tile([P, P], F32, name="ident")
         make_identity(nc, ident[:])
+        minus_one = keep.tile([P, V], F32, name="minus_one")
+        nc.gpsimd.memset(minus_one[:], -1.0)
 
+        last = PIECES - 1
         grouped = [keep.tile([P, PIECE, PACK], BF16, name=f"grouped{c}", tag=f"grouped{c}", align_bytes=64) for c in range(PIECES)]
         half = S // 2
         front = keep.tile([P, 2, half], BF16, name="front")
-        back = keep.tile([P, PIECES, 2, PIECE], BF16, name="back")
+        back = keep.tile([P, last, 2, PIECE], BF16, name="back")
         for j in range(2):
             rounded = keep.tile([P, T], BF16, name=f"rounded{j}")
             nc.scalar.copy(rounded[:, 0:CAST_SPLIT], planes[j][:, 0:CAST_SPLIT])
@@ -82,17 +90,13 @@ def tile_picked_huber_none_e_kernel(
                 nc.scalar.activation(grouped[c][:, :, j], rounded[:].indirect(entries(picked, PIECE * c, PIECE)), COPY)
         for c in range(2):
             nc.scalar.copy(grouped[c][:, :, 0:2], front[:, :, c * PIECE : (c + 1) * PIECE].rearrange("p j s -> p s j"))
-        nc.vector.tensor_copy(back[:, :, 0, :], planes[2][:].indirect(picked[:]))
-        runs = [(0, 0, PIECE // 2), (0, PIECE // 2, PIECE // 2)] + [(c, 0, PIECE) for c in range(1, PIECES)]
-        for c, first, count in runs:
-            nc.vector.tensor_copy(
-                back[:, c, 1, first : first + count], planes[3][:].indirect(entries(picked, PIECE * c + first, count))
-            )
-        for c, first, count in runs[:-1]:
-            nc.scalar.copy(
-                grouped[c][:, first : first + count, 2:4],
-                back[:, c, :, first : first + count].rearrange("p j s -> p s j"),
-            )
+        nc.vector.tensor_copy(back[:, :, 0, :], planes[2][:].indirect(entries(picked, 0, last * PIECE)))
+        nc.vector.tensor_copy(grouped[last][:, :, 2], planes[2][:].indirect(entries(picked, last * PIECE, PIECE)))
+        for c in range(PIECES):
+            target = grouped[c][:, :, 3] if c == last else back[:, c, 1, :]
+            nc.vector.tensor_copy(target, planes[3][:].indirect(entries(picked, PIECE * c, PIECE)))
+        for c in range(last):
+            nc.scalar.copy(grouped[c][:, :, 2:4], back[:, c].rearrange("p j s -> p s j"))
 
         y = keep.tile([P, S], F32, name="y")
 
@@ -112,55 +116,66 @@ def tile_picked_huber_none_e_kernel(
             else:
                 nc.scalar.copy(y[:, c * PIECE : (c + 1) * PIECE], acc[:])
 
-        last = PIECES - 1
-        project(0)
-        nc.vector.tensor_copy(grouped[last][:, :, 2:4], back[:, last].rearrange("p j s -> p s j"))
-        project(1)
-        project(last)
-        project(2)
+        for c in (0, 1, last, 2):
+            project(c)
 
         halves = [slice(h * P, (h + 1) * P) for h in range(HALVES)]
-        lower = keep.tile([P, HALVES], F32, name="lower", tag="grouped2", align_bytes=64)
-        nc.vector.tensor_scalar(lower[:], upper[:], -1.0, None, ALU.mult)
-        yc = keep.tile([P, V], F32, name="yc")
-        for h in range(HALVES):
-            nc.vector.tensor_copy(yc[:, halves[h]], y[:].indirect(entries(centre, h * P, P)))
+        whole = slice(0, V)
+        limits = keep.tile([P, V + 2 * HALVES], F32, name="limits", tag="grouped2", align_bytes=64)
+        floor = limits[:, 0:V]
+        half_reach = limits[:, V : V + HALVES]
+        base_shift = limits[:, V + HALVES : V + 2 * HALVES]
+        nc.vector.tensor_scalar(floor, reach[:], -2.0, None, ALU.mult)
+        nc.vector.tensor_scalar(half_reach, reach_t[:], 2.0 / D, None, ALU.mult)
+        nc.vector.tensor_scalar(base_shift, reach_t[:], -2.0 * TURNED / D, None, ALU.mult)
 
-        early = [bank(6 + h, 2 * P) for h in range(HALVES)]
-        turned = {(d, h): early[h][:, d * P : (d + 1) * P] for d in range(2) for h in range(HALVES)}
-        for d in range(2, D):
-            for h in range(HALVES):
-                turned[(d, h)] = bank(2 * (d - 2) + h, P)[:]
-        totals = [bank(4 + h, P) for h in range(HALVES)]
-
-        def pull(d, first, count):
-            diff = keep.tile([P, count * P], F32, name=f"diff{d}_{first}")
-            cols = slice(first * P, (first + count) * P)
-            nc.vector.tensor_tensor(diff[:], y[:].indirect(entries(near[d], first * P, count * P)), yc[:, cols], ALU.subtract)
-            for i in range(count):
-                h = first + i
-                nc.tensor.transpose(turned[(d, h)], diff[:, i * P : (i + 1) * P], ident[:])
-
-        def clip(h, source, first, count):
-            clipped = keep.tile([P, count * P], F32, name=f"clipped{h}_{first}")
-            nc.vector.tensor_scalar(clipped[:], source, upper[:, h : h + 1], lower[:, h : h + 1], ALU.min, ALU.max)
-            for i in range(count):
-                d = first + i
-                nc.tensor.matmul(
-                    totals[h][:], lhsT=clipped[:, i * P : (i + 1) * P], rhs=ident[:],
-                    start=(d == 0), stop=(d == D - 1), is_transpose=True,
-                )
-
-        pull(0, 0, 1)
-        pull(0, 1, 1)
-        pull(1, 0, 2)
-        pull(2, 0, 2)
-        pull(3, 0, 1)
-        pull(3, 1, 1)
+        top = keep.tile([P, V], F32, name="top")
+        nc.vector.tensor_tensor(top[:], y[:].indirect(centre[:]), reach[:], ALU.add)
+        fetched = [keep.tile([P, V], F32, name=f"fetched{d}") for d in range(D)]
         for d in range(D):
+            if d == 0:
+                nc.vector.tensor_tensor(fetched[d][:], y[:].indirect(near[d][:]), minus_one[:], ALU.mult)
+            else:
+                nc.vector.tensor_tensor(fetched[d][:], y[:].indirect(near[d][:]), top[:], ALU.subtract)
+        totals = [bank(6 + h, P) for h in range(HALVES)]
+
+        def turn(target, source, first, final):
+            nc.tensor.matmul(target[:], lhsT=source, rhs=ident[:], start=first, stop=final, is_transpose=True)
+
+        for h in range(HALVES):
+            turned = bank(4 + h, P)
+            turn(turned, top[:, halves[h]], True, True)
+            base = keep.tile([P, P], F32, name=f"base{h}")
+            nc.scalar.activation(base[:], turned[:], IDENTITY, bias=base_shift[:, h : h + 1])
+            turn(totals[h], base[:], True, False)
+        for d in range(TURNED):
+            room = [bank(HALVES * d + h, P) for h in range(HALVES)]
+            if d == 0:
+                for h in range(HALVES):
+                    turn(room[h], top[:, halves[h]], True, False)
+            short = []
             for h in range(HALVES):
-                clip(h, turned[(d, h)], d, 1)
+                turn(room[h], fetched[d][:, halves[h]], d > 0, True)
+                under = keep.tile([P, P], F32, name=f"under{d}_{h}")
+                nc.scalar.activation(under[:], room[h][:], RELU, scale=1.0 if d == 0 else -1.0)
+                short.append(under)
+            for h in range(HALVES):
+                pull = keep.tile([P, P], F32, name=f"pull{d}_{h}")
+                nc.scalar.activation(pull[:], short[h][:], RELU, bias=half_reach[:, h : h + 1], scale=-1.0 / D)
+                turn(totals[h], pull[:], False, d == TURNED - 1)
+
+        clipped = [keep.tile([P, V], F32, name=f"clipped{d}") for d in range(TURNED, D)]
+
+        def clip(d, cols):
+            nc.vector.scalar_tensor_tensor(clipped[d - TURNED][:, cols], fetched[d][:, cols], 0.0, floor[:, cols], ALU.min, ALU.max)
+
+        clip(2, whole)
+        for h in range(HALVES):
+            clip(3, halves[h])
+        both = keep.tile([P, V], F32, name="both")
+        for h in range(HALVES):
+            nc.vector.tensor_tensor(both[:, halves[h]], clipped[0][:, halves[h]], clipped[1][:, halves[h]], ALU.add)
         for h in range(HALVES):
             res = keep.tile([P, P], F32, name=f"res{h}")
-            nc.vector.scalar_tensor_tensor(res[:], totals[h][:], 1.0 / D, yc[:, halves[h]], ALU.mult, ALU.add)
+            nc.vector.scalar_tensor_tensor(res[:], both[:, halves[h]], 1.0 / D, totals[h][:], ALU.mult, ALU.add)
             nc.sync.dma_start(out[:, halves[h]], res[:])

@@ -80,28 +80,35 @@ def tile_picked_huber_none_e_kernel(
         grouped = [keep.tile([P, PIECE, PACK], BF16, name=f"grouped{c}", tag=f"grouped{c}", align_bytes=64) for c in range(PIECES)]
         half = S // 2
         front = keep.tile([P, 2, half], BF16, name="front")
-        back = keep.tile([P, last, 2, PIECE], BF16, name="back")
+        pairs_first = keep.tile([P, 1, 2, PIECE, 2], BF16, name="pairs_first", tag="back_first", align_bytes=64)
+        pairs_rest = keep.tile([P, last - 1, 2, PIECE, 2], BF16, name="pairs_rest")
+        pairs = [pairs_first[:, 0]] + [pairs_rest[:, c] for c in range(last - 1)]
         for j in range(2):
             rounded = keep.tile([P, T], BF16, name=f"rounded{j}")
             nc.scalar.copy(rounded[:, 0:CAST_SPLIT], planes[j][:, 0:CAST_SPLIT])
             nc.vector.tensor_copy(rounded[:, CAST_SPLIT:T], planes[j][:, CAST_SPLIT:T])
             nc.vector.tensor_copy(front[:, j, :], planes[j][:].indirect(entries(picked, 0, half)))
             for c in range(2, PIECES):
-                nc.scalar.activation(grouped[c][:, :, j], rounded[:].indirect(entries(picked, PIECE * c, PIECE)), COPY)
+                target = grouped[c][:, :, j] if c == last else pairs[c][:, 0, :, j]
+                nc.scalar.activation(target, rounded[:].indirect(entries(picked, PIECE * c, PIECE)), COPY)
         for c in range(2):
-            nc.scalar.copy(grouped[c][:, :, 0:2], front[:, :, c * PIECE : (c + 1) * PIECE].rearrange("p j s -> p s j"))
-        nc.vector.tensor_copy(back[:, :, 0, :], planes[2][:].indirect(entries(picked, 0, last * PIECE)))
+            nc.scalar.copy(pairs[c][:, 0], front[:, :, c * PIECE : (c + 1) * PIECE].rearrange("p j s -> p s j"))
+        nc.vector.tensor_copy(pairs_first[:, :, 1, :, 0], planes[2][:].indirect(entries(picked, 0, PIECE)))
+        nc.vector.tensor_copy(pairs_rest[:, :, 1, :, 0], planes[2][:].indirect(entries(picked, PIECE, (last - 1) * PIECE)))
         nc.vector.tensor_copy(grouped[last][:, :, 2], planes[2][:].indirect(entries(picked, last * PIECE, PIECE)))
         for c in range(PIECES):
-            target = grouped[c][:, :, 3] if c == last else back[:, c, 1, :]
+            target = grouped[c][:, :, 3] if c == last else pairs[c][:, 1, :, 1]
             nc.vector.tensor_copy(target, planes[3][:].indirect(entries(picked, PIECE * c, PIECE)))
         for c in range(last):
-            nc.scalar.copy(grouped[c][:, :, 2:4], back[:, c].rearrange("p j s -> p s j"))
+            nc.scalar.copy(
+                grouped[c][:].rearrange("p s j -> p (s j)").bitcast(U32).rearrange("p (s u) -> p s u", u=2),
+                pairs[c].rearrange("p u s e -> p u (s e)").bitcast(U32).rearrange("p u s -> p s u"),
+            )
 
         y = keep.tile([P, S], F32, name="y")
 
         def project(c):
-            codes = keep.tile([P, PIECE], U32, name=f"codes{c}", align_bytes=64)
+            codes = keep.tile([P, PIECE], U32, name=f"codes{c}", tag="back_first" if c == last else f"codes{c}", align_bytes=64)
             scales = keep.tile([P, PIECE], U8, name=f"scales{c}", align_bytes=64)
             nc.vector.quantize_mx(
                 out=codes[:].bitcast(FP8X4), scales=scales[:], in_=grouped[c][:].rearrange("p s j -> p (s j)")
@@ -116,7 +123,7 @@ def tile_picked_huber_none_e_kernel(
             else:
                 nc.scalar.copy(y[:, c * PIECE : (c + 1) * PIECE], acc[:])
 
-        for c in (0, 1, last, 2):
+        for c in (0, last, 1, 2):
             project(c)
 
         halves = [slice(h * P, (h + 1) * P) for h in range(HALVES)]

@@ -26,7 +26,8 @@ PIECES = S // PIECE
 HALVES = V // P
 LANE = 16
 TURNED = 2
-CAST_SPLIT = 256
+CAST_SPLIT = 768
+LOAD_ORDER = (0, 2, 1, 3)
 
 
 def entries(offsets, first, count):
@@ -48,9 +49,9 @@ def tile_picked_huber_none_e_kernel(
         rows = xT.rearrange("(p j) t -> j p t", j=PACK)
         planes = [keep.tile([P, T], F32, name=f"plane{j}") for j in range(PACK)]
         picked = keep.tile([P, S // LANE], U16, name="picked")
-        nc.sync.dma_start(planes[0][:], rows[0])
+        nc.sync.dma_start(planes[LOAD_ORDER[0]][:], rows[LOAD_ORDER[0]])
         nc.sync.dma_start(picked[:], offs)
-        for j in range(1, PACK):
+        for j in LOAD_ORDER[1:]:
             nc.sync.dma_start(planes[j][:], rows[j])
         reach = keep.tile([P, V], F32, name="reach")
         nc.sync.dma_start(reach[:], bound)
@@ -78,53 +79,57 @@ def tile_picked_huber_none_e_kernel(
 
         last = PIECES - 1
         grouped = [keep.tile([P, PIECE, PACK], BF16, name=f"grouped{c}", tag=f"grouped{c}", align_bytes=64) for c in range(PIECES)]
-        half = S // 2
-        front = keep.tile([P, 2, half], BF16, name="front")
-        pairs_first = keep.tile([P, 1, 2, PIECE, 2], BF16, name="pairs_first", tag="back_first", align_bytes=64)
-        pairs_rest = keep.tile([P, last - 1, 2, PIECE, 2], BF16, name="pairs_rest")
-        pairs = [pairs_first[:, 0]] + [pairs_rest[:, c] for c in range(last - 1)]
-        for j in range(2):
+        early = keep.tile([P, 2, 2, PIECE, 2], BF16, name="early", tag="early", align_bytes=64)
+        third = keep.tile([P, 2, PIECE, 2], BF16, name="third")
+        pairs = [early[:, 0], early[:, 1], third[:]]
+
+        def slots(j):
+            return [
+                (early[:, :, j // 2, :, j % 2], entries(picked, 0, 2 * PIECE)),
+                (third[:, j // 2, :, j % 2], entries(picked, 2 * PIECE, PIECE)),
+                (grouped[last][:, :, j], entries(picked, last * PIECE, PIECE)),
+            ]
+
+        for j in LOAD_ORDER:
+            if j >= 2:
+                for target, offsets in slots(j):
+                    nc.vector.tensor_copy(target, planes[j][:].indirect(offsets))
+                continue
             rounded = keep.tile([P, T], BF16, name=f"rounded{j}")
-            nc.scalar.copy(rounded[:, 0:CAST_SPLIT], planes[j][:, 0:CAST_SPLIT])
-            nc.vector.tensor_copy(rounded[:, CAST_SPLIT:T], planes[j][:, CAST_SPLIT:T])
-            nc.vector.tensor_copy(front[:, j, :], planes[j][:].indirect(entries(picked, 0, half)))
-            for c in range(2, PIECES):
-                target = grouped[c][:, :, j] if c == last else pairs[c][:, 0, :, j]
-                nc.scalar.activation(target, rounded[:].indirect(entries(picked, PIECE * c, PIECE)), COPY)
-        for c in range(2):
-            nc.scalar.copy(pairs[c][:, 0], front[:, :, c * PIECE : (c + 1) * PIECE].rearrange("p j s -> p s j"))
-        nc.vector.tensor_copy(pairs_first[:, :, 1, :, 0], planes[2][:].indirect(entries(picked, 0, PIECE)))
-        nc.vector.tensor_copy(pairs_rest[:, :, 1, :, 0], planes[2][:].indirect(entries(picked, PIECE, (last - 1) * PIECE)))
-        nc.vector.tensor_copy(grouped[last][:, :, 2], planes[2][:].indirect(entries(picked, last * PIECE, PIECE)))
-        for c in range(PIECES):
-            target = grouped[c][:, :, 3] if c == last else pairs[c][:, 1, :, 1]
-            nc.vector.tensor_copy(target, planes[3][:].indirect(entries(picked, PIECE * c, PIECE)))
-        for c in range(last):
-            nc.scalar.copy(
-                grouped[c][:].rearrange("p s j -> p (s j)").bitcast(U32).rearrange("p (s u) -> p s u", u=2),
-                pairs[c].rearrange("p u s e -> p u (s e)").bitcast(U32).rearrange("p u s -> p s u"),
-            )
+            if j == 0:
+                nc.scalar.copy(rounded[:], planes[j][:])
+            else:
+                nc.scalar.copy(rounded[:, 0:CAST_SPLIT], planes[j][:, 0:CAST_SPLIT])
+                nc.vector.tensor_copy(rounded[:, CAST_SPLIT:T], planes[j][:, CAST_SPLIT:T])
+            (target, offsets), *rest = slots(j)
+            nc.vector.tensor_copy(target, planes[j][:].indirect(offsets))
+            for target, offsets in rest:
+                nc.scalar.activation(target, rounded[:].indirect(offsets), COPY)
+        runs = [(0, 0, PIECE), (1, 0, PIECE), (last, 0, PIECE), (2, 0, PIECE // 2), (2, PIECE // 2, PIECE // 2)]
+        for c, first, count in runs:
+            if c != last:
+                words = grouped[c][:].rearrange("p s j -> p (s j)").bitcast(U32).rearrange("p (s u) -> p s u", u=2)
+                halves_of = pairs[c].rearrange("p u s e -> p u (s e)").bitcast(U32).rearrange("p u s -> p s u")
+                nc.scalar.copy(words[:, first : first + count], halves_of[:, first : first + count])
 
         y = keep.tile([P, S], F32, name="y")
-
-        def project(c):
-            codes = keep.tile([P, PIECE], U32, name=f"codes{c}", tag="back_first" if c == last else f"codes{c}", align_bytes=64)
-            scales = keep.tile([P, PIECE], U8, name=f"scales{c}", align_bytes=64)
+        for i, (c, first, count) in enumerate(runs):
+            codes = keep.tile([P, count], U32, name=f"codes{i}", tag="early" if c == last else f"codes{i}", align_bytes=64)
+            scales = keep.tile([P, count], U8, name=f"scales{i}", align_bytes=64)
             nc.vector.quantize_mx(
-                out=codes[:].bitcast(FP8X4), scales=scales[:], in_=grouped[c][:].rearrange("p s j -> p (s j)")
+                out=codes[:].bitcast(FP8X4), scales=scales[:],
+                in_=grouped[c][:, first : first + count].rearrange("p s j -> p (s j)"),
             )
-            acc = bank(c, PIECE)
+            acc = bank(i, count)
             nc.tensor.matmul_mx(
                 out=acc[:], lhsT=w_codes[:].bitcast(FP8X4), lhsT_scale=w_scales[:],
                 rhs=codes[:].bitcast(FP8X4), rhs_scale=scales[:], start=True, stop=True,
             )
-            if c == 2:
-                nc.vector.tensor_copy(y[:, c * PIECE : (c + 1) * PIECE], acc[:])
+            cols = slice(c * PIECE + first, c * PIECE + first + count)
+            if i == len(runs) - 1:
+                nc.vector.tensor_copy(y[:, cols], acc[:])
             else:
-                nc.scalar.copy(y[:, c * PIECE : (c + 1) * PIECE], acc[:])
-
-        for c in (0, last, 1, 2):
-            project(c)
+                nc.scalar.copy(y[:, cols], acc[:])
 
         halves = [slice(h * P, (h + 1) * P) for h in range(HALVES)]
         whole = slice(0, V)

@@ -63,9 +63,6 @@ def tile_picked_huber_none_e_kernel(
             nc.sync.dma_start(
                 w_scales[32 * q : 32 * q + 4, :].bitcast(I32), w1_scales[0, 4 * q : 4 * q + 4, :].bitcast(I32)
             )
-        reach_t = keep.tile([P, HALVES], F32, name="reach_t")
-        with nc.allow_non_contiguous_dma(reason="one bound for each partition"):
-            nc.sync.dma_start(reach_t[:], bound[0:1, :].rearrange("o (h p) -> p (o h)", p=P))
         near = []
         for d, pos in enumerate((pos1, pos2, pos3, pos4)):
             lst = keep.tile([P, V // LANE], U16, name=f"near{d}")
@@ -76,6 +73,11 @@ def tile_picked_huber_none_e_kernel(
         make_identity(nc, ident[:])
         minus_one = keep.tile([P, V], F32, name="minus_one")
         nc.gpsimd.memset(minus_one[:], -1.0)
+
+        reach_turned = bank(6, V)
+        for h in range(HALVES):
+            nc.tensor.transpose(reach_turned[:, h * P : (h + 1) * P], reach[:, h * P : (h + 1) * P], ident[:])
+        reach_t = reach_turned[:, 0:V:P]
 
         last = PIECES - 1
         grouped = [keep.tile([P, PIECE, PACK], BF16, name=f"grouped{c}", tag=f"grouped{c}", align_bytes=64) for c in range(PIECES)]
@@ -138,8 +140,8 @@ def tile_picked_huber_none_e_kernel(
         half_reach = limits[:, V : V + HALVES]
         base_shift = limits[:, V + HALVES : V + 2 * HALVES]
         nc.vector.tensor_scalar(floor, reach[:], -2.0, None, ALU.mult)
-        nc.vector.tensor_scalar(half_reach, reach_t[:], 2.0 / D, None, ALU.mult)
-        nc.vector.tensor_scalar(base_shift, reach_t[:], -2.0 * TURNED / D, None, ALU.mult)
+        nc.vector.tensor_scalar(half_reach, reach_t, 2.0 / D, None, ALU.mult)
+        nc.vector.tensor_scalar(base_shift, reach_t, -2.0 * TURNED / D, None, ALU.mult)
 
         top = keep.tile([P, V], F32, name="top")
         nc.vector.tensor_tensor(top[:], y[:].indirect(centre[:]), reach[:], ALU.add)

@@ -25,7 +25,7 @@ PIECE = 128
 PIECES = S // PIECE
 HALVES = V // P
 LANE = 16
-TURNED = 2
+TURNED = (3, 2)
 CAST_SPLIT = 768
 LOAD_ORDER = (0, 2, 1, 3)
 
@@ -77,7 +77,10 @@ def tile_picked_huber_none_e_kernel(
         reach_turned = bank(6, V)
         for h in range(HALVES):
             nc.tensor.transpose(reach_turned[:, h * P : (h + 1) * P], reach[:, h * P : (h + 1) * P], ident[:])
-        reach_t = reach_turned[:, 0:V:P]
+        factors = keep.tile([P, HALVES, 2], F32, name="factors")
+        nc.gpsimd.memset(factors[:, :, 0:1], 2.0 / D)
+        for h in range(HALVES):
+            nc.gpsimd.memset(factors[:, h, 1:2], -2.0 * TURNED[h] / D)
 
         last = PIECES - 1
         grouped = [keep.tile([P, PIECE, PACK], BF16, name=f"grouped{c}", tag=f"grouped{c}", align_bytes=64) for c in range(PIECES)]
@@ -134,23 +137,19 @@ def tile_picked_huber_none_e_kernel(
                 nc.scalar.copy(y[:, cols], acc[:])
 
         halves = [slice(h * P, (h + 1) * P) for h in range(HALVES)]
-        whole = slice(0, V)
         limits = keep.tile([P, V + 2 * HALVES], F32, name="limits", tag="grouped2", align_bytes=64)
         floor = limits[:, 0:V]
-        half_reach = limits[:, V : V + HALVES]
-        base_shift = limits[:, V + HALVES : V + 2 * HALVES]
+        biases = limits[:, V : V + 2 * HALVES].rearrange("p (h u) -> p h u", u=2)
         nc.vector.tensor_scalar(floor, reach[:], -2.0, None, ALU.mult)
-        nc.vector.tensor_scalar(half_reach, reach_t, 2.0 / D, None, ALU.mult)
-        nc.vector.tensor_scalar(base_shift, reach_t, -2.0 * TURNED / D, None, ALU.mult)
+        nc.vector.tensor_tensor(biases, reach_turned[:].rearrange("p (h m) -> p h m", m=P)[:, :, 0:2], factors[:], ALU.mult)
 
         top = keep.tile([P, V], F32, name="top")
         nc.vector.tensor_tensor(top[:], y[:].indirect(centre[:]), reach[:], ALU.add)
         fetched = [keep.tile([P, V], F32, name=f"fetched{d}") for d in range(D)]
-        for d in range(D):
-            if d == 0:
-                nc.vector.tensor_tensor(fetched[d][:], y[:].indirect(near[d][:]), minus_one[:], ALU.mult)
-            else:
-                nc.vector.tensor_tensor(fetched[d][:], y[:].indirect(near[d][:]), top[:], ALU.subtract)
+        nc.vector.tensor_tensor(fetched[0][:], y[:].indirect(near[0][:]), minus_one[:], ALU.mult)
+        for d, cols in ((1, slice(0, V)), (2, halves[0]), (2, halves[1]), (3, slice(0, V))):
+            looked_up = y[:].indirect(entries(near[d], cols.start, cols.stop - cols.start))
+            nc.vector.tensor_tensor(fetched[d][:, cols], looked_up, top[:, cols], ALU.subtract)
         totals = [bank(6 + h, P) for h in range(HALVES)]
 
         def turn(target, source, first, final):
@@ -160,36 +159,35 @@ def tile_picked_huber_none_e_kernel(
             turned = bank(4 + h, P)
             turn(turned, top[:, halves[h]], True, True)
             base = keep.tile([P, P], F32, name=f"base{h}")
-            nc.scalar.activation(base[:], turned[:], IDENTITY, bias=base_shift[:, h : h + 1])
+            nc.scalar.activation(base[:], turned[:], IDENTITY, bias=biases[:, h, 1:2])
             turn(totals[h], base[:], True, False)
-        for d in range(TURNED):
-            room = [bank(HALVES * d + h, P) for h in range(HALVES)]
+        for d in range(max(TURNED)):
+            turned_halves = [h for h in range(HALVES) if d < TURNED[h]]
+            room = {h: bank(HALVES * d + h, P) for h in turned_halves}
             if d == 0:
-                for h in range(HALVES):
+                for h in turned_halves:
                     turn(room[h], top[:, halves[h]], True, False)
-            short = []
-            for h in range(HALVES):
+            short = {}
+            for h in turned_halves:
                 turn(room[h], fetched[d][:, halves[h]], d > 0, True)
-                under = keep.tile([P, P], F32, name=f"under{d}_{h}")
-                nc.scalar.activation(under[:], room[h][:], RELU, scale=1.0 if d == 0 else -1.0)
-                short.append(under)
-            for h in range(HALVES):
+                short[h] = keep.tile([P, P], F32, name=f"under{d}_{h}")
+                nc.scalar.activation(short[h][:], room[h][:], RELU, scale=1.0 if d == 0 else -1.0)
+            for h in turned_halves:
                 pull = keep.tile([P, P], F32, name=f"pull{d}_{h}")
-                nc.scalar.activation(pull[:], short[h][:], RELU, bias=half_reach[:, h : h + 1], scale=-1.0 / D)
-                turn(totals[h], pull[:], False, d == TURNED - 1)
+                nc.scalar.activation(pull[:], short[h][:], RELU, bias=biases[:, h, 0:1], scale=-1.0 / D)
+                turn(totals[h], pull[:], False, d == TURNED[h] - 1)
 
-        clipped = [keep.tile([P, V], F32, name=f"clipped{d}") for d in range(TURNED, D)]
+        def clip(d, h):
+            clipped = keep.tile([P, P], F32, name=f"clipped{d}_{h}")
+            nc.vector.scalar_tensor_tensor(clipped[:], fetched[d][:, halves[h]], 0.0, floor[:, halves[h]], ALU.min, ALU.max)
+            return clipped
 
-        def clip(d, cols):
-            nc.vector.scalar_tensor_tensor(clipped[d - TURNED][:, cols], fetched[d][:, cols], 0.0, floor[:, cols], ALU.min, ALU.max)
-
-        clip(2, whole)
-        for h in range(HALVES):
-            clip(3, halves[h])
-        both = keep.tile([P, V], F32, name="both")
-        for h in range(HALVES):
-            nc.vector.tensor_tensor(both[:, halves[h]], clipped[0][:, halves[h]], clipped[1][:, halves[h]], ALU.add)
-        for h in range(HALVES):
+        third_1 = clip(2, 1)
+        fourth_1 = clip(3, 1)
+        fourth_0 = clip(3, 0)
+        both = keep.tile([P, P], F32, name="both")
+        nc.vector.tensor_tensor(both[:], third_1[:], fourth_1[:], ALU.add)
+        for h, rest in ((0, fourth_0), (1, both)):
             res = keep.tile([P, P], F32, name=f"res{h}")
-            nc.vector.scalar_tensor_tensor(res[:], both[:, halves[h]], 1.0 / D, totals[h][:], ALU.mult, ALU.add)
+            nc.vector.scalar_tensor_tensor(res[:], rest[:], 1.0 / D, totals[h][:], ALU.mult, ALU.add)
             nc.sync.dma_start(out[:, halves[h]], res[:])

@@ -162,7 +162,7 @@ def tile_picked_huber_none_e_kernel(
             nc.scalar.activation(base[:], turned[:], IDENTITY, bias=biases[:, h, 1:2])
             turn(totals[h], base[:], True, False)
         for d in range(max(TURNED)):
-            turned_halves = [h for h in range(HALVES) if d < TURNED[h]]
+            turned_halves = sorted((h for h in range(HALVES) if d < TURNED[h]), key=lambda h: TURNED[h])
             room = {h: bank(HALVES * d + h, P) for h in turned_halves}
             if d == 0:
                 for h in turned_halves:
@@ -182,12 +182,14 @@ def tile_picked_huber_none_e_kernel(
             nc.vector.scalar_tensor_tensor(clipped[:], fetched[d][:, halves[h]], 0.0, floor[:, halves[h]], ALU.min, ALU.max)
             return clipped
 
+        def add_share(name, clipped, rest):
+            res = keep.tile([P, P], F32, name=name)
+            nc.vector.scalar_tensor_tensor(res[:], clipped[:], 1.0 / D, rest[:], ALU.mult, ALU.add)
+            return res
+
         third_1 = clip(2, 1)
         fourth_1 = clip(3, 1)
+        partial_1 = add_share("partial_1", third_1, totals[1])
         fourth_0 = clip(3, 0)
-        both = keep.tile([P, P], F32, name="both")
-        nc.vector.tensor_tensor(both[:], third_1[:], fourth_1[:], ALU.add)
-        for h, rest in ((0, fourth_0), (1, both)):
-            res = keep.tile([P, P], F32, name=f"res{h}")
-            nc.vector.scalar_tensor_tensor(res[:], rest[:], 1.0 / D, totals[h][:], ALU.mult, ALU.add)
-            nc.sync.dma_start(out[:, halves[h]], res[:])
+        nc.sync.dma_start(out[:, halves[1]], add_share("res1", fourth_1, partial_1)[:])
+        nc.sync.dma_start(out[:, halves[0]], add_share("res0", fourth_0, totals[0])[:])

@@ -55,14 +55,14 @@ def tile_picked_huber_none_e_kernel(
             nc.sync.dma_start(planes[j][:], rows[j])
         reach = keep.tile([P, V], F32, name="reach")
         nc.sync.dma_start(reach[:], bound)
-        centre = keep.tile([P, V // LANE], U16, name="centre")
-        nc.sync.dma_start(centre[:], cen)
         w_codes = keep.tile([P, N], U32, name="w_codes", align_bytes=64)
         nc.sync.dma_start(w_codes[:].bitcast(I32), w1_words[0].rearrange("p n t -> p (n t)").bitcast(I32))
         for q in range(4):
             nc.sync.dma_start(
                 w_scales[32 * q : 32 * q + 4, :].bitcast(I32), w1_scales[0, 4 * q : 4 * q + 4, :].bitcast(I32)
             )
+        centre = keep.tile([P, V // LANE], U16, name="centre")
+        nc.sync.dma_start(centre[:], cen)
         near = []
         for d, pos in enumerate((pos1, pos2, pos3, pos4)):
             lst = keep.tile([P, V // LANE], U16, name=f"near{d}")
@@ -131,7 +131,7 @@ def tile_picked_huber_none_e_kernel(
                 rhs=codes[:].bitcast(FP8X4), rhs_scale=scales[:], start=True, stop=True,
             )
             cols = slice(c * PIECE + first, c * PIECE + first + count)
-            if i == len(runs) - 1:
+            if i % 2 == 1:
                 nc.vector.tensor_copy(y[:, cols], acc[:])
             else:
                 nc.scalar.copy(y[:, cols], acc[:])

@@ -147,7 +147,7 @@ def tile_picked_huber_none_e_kernel(
         nc.vector.tensor_tensor(top[:], y[:].indirect(centre[:]), reach[:], ALU.add)
         fetched = [keep.tile([P, V], F32, name=f"fetched{d}") for d in range(D)]
         nc.vector.tensor_tensor(fetched[0][:], y[:].indirect(near[0][:]), minus_one[:], ALU.mult)
-        for d, cols in ((1, slice(0, V)), (2, halves[0]), (2, halves[1]), (3, slice(0, V))):
+        for d, cols in ((1, halves[1]), (1, halves[0]), (2, halves[0]), (2, halves[1]), (3, slice(0, V))):
             looked_up = y[:].indirect(entries(near[d], cols.start, cols.stop - cols.start))
             nc.vector.tensor_tensor(fetched[d][:, cols], looked_up, top[:, cols], ALU.subtract)
         totals = [bank(6 + h, P) for h in range(HALVES)]

@@ -26,7 +26,7 @@ PIECES = S // PIECE
 HALVES = V // P
 LANE = 16
 TURNED = (3, 2)
-CAST_SPLIT = 768
+CAST_SPLIT = 704
 LOAD_ORDER = (0, 2, 1, 3)
 
 
@@ -84,14 +84,12 @@ def tile_picked_huber_none_e_kernel(
 
         last = PIECES - 1
         grouped = [keep.tile([P, PIECE, PACK], BF16, name=f"grouped{c}", tag=f"grouped{c}", align_bytes=64) for c in range(PIECES)]
-        early = keep.tile([P, 2, 2, PIECE, 2], BF16, name="early", tag="early", align_bytes=64)
-        third = keep.tile([P, 2, PIECE, 2], BF16, name="third")
-        pairs = [early[:, 0], early[:, 1], third[:]]
+        paired = keep.tile([P, last, 2, PIECE, 2], BF16, name="paired")
+        pairs = [paired[:, c] for c in range(last)]
 
         def slots(j):
-            return [
-                (early[:, :, j // 2, :, j % 2], entries(picked, 0, 2 * PIECE)),
-                (third[:, j // 2, :, j % 2], entries(picked, 2 * PIECE, PIECE)),
+            cuts = ((0, last),) if j == 2 else ((0, 2), (2, last))
+            return [(paired[:, a:b, j // 2, :, j % 2], entries(picked, a * PIECE, (b - a) * PIECE)) for a, b in cuts] + [
                 (grouped[last][:, :, j], entries(picked, last * PIECE, PIECE)),
             ]
 
@@ -119,7 +117,7 @@ def tile_picked_huber_none_e_kernel(
 
         y = keep.tile([P, S], F32, name="y")
         for i, (c, first, count) in enumerate(runs):
-            codes = keep.tile([P, count], U32, name=f"codes{i}", tag="early" if c == last else f"codes{i}", align_bytes=64)
+            codes = keep.tile([P, count], U32, name=f"codes{i}", tag="grouped0" if c == last else f"codes{i}", align_bytes=64)
             scales = keep.tile([P, count], U8, name=f"scales{i}", align_bytes=64)
             nc.vector.quantize_mx(
                 out=codes[:].bitcast(FP8X4), scales=scales[:],
@@ -155,7 +153,10 @@ def tile_picked_huber_none_e_kernel(
         def turn(target, source, first, final):
             nc.tensor.matmul(target[:], lhsT=source, rhs=ident[:], start=first, stop=final, is_transpose=True)
 
-        for h in range(HALVES):
+        first_room = {h: bank(h, P) for h in reversed(range(HALVES))}
+        for h in first_room:
+            turn(first_room[h], top[:, halves[h]], True, False)
+        for h in first_room:
             turned = bank(4 + h, P)
             turn(turned, top[:, halves[h]], True, True)
             base = keep.tile([P, P], F32, name=f"base{h}")
@@ -163,10 +164,7 @@ def tile_picked_huber_none_e_kernel(
             turn(totals[h], base[:], True, False)
         for d in range(max(TURNED)):
             turned_halves = sorted((h for h in range(HALVES) if d < TURNED[h]), key=lambda h: TURNED[h])
-            room = {h: bank(HALVES * d + h, P) for h in turned_halves}
-            if d == 0:
-                for h in turned_halves:
-                    turn(room[h], top[:, halves[h]], True, False)
+            room = first_room if d == 0 else {h: bank(HALVES * d + h, P) for h in turned_halves}
             short = {}
             for h in turned_halves:
                 turn(room[h], fetched[d][:, halves[h]], d > 0, True)

@@ -17,7 +17,6 @@ FP8X4 = mybir.dt.float8_e4m3fn_x4
 ALU = mybir.AluOpType
 COPY = mybir.ActivationFunctionType.Copy
 RELU = mybir.ActivationFunctionType.Relu
-IDENTITY = mybir.ActivationFunctionType.Identity
 
 P = 128
 PACK = 4
@@ -25,7 +24,7 @@ PIECE = 128
 PIECES = S // PIECE
 HALVES = V // P
 LANE = 16
-TURNED = (3, 2)
+TURNED = 2
 CAST_SPLIT = 704
 LOAD_ORDER = (0, 2, 1, 3)
 
@@ -57,30 +56,31 @@ def tile_picked_huber_none_e_kernel(
         nc.sync.dma_start(reach[:], bound)
         w_codes = keep.tile([P, N], U32, name="w_codes", align_bytes=64)
         nc.sync.dma_start(w_codes[:].bitcast(I32), w1_words[0].rearrange("p n t -> p (n t)").bitcast(I32))
-        for q in range(4):
-            nc.sync.dma_start(
-                w_scales[32 * q : 32 * q + 4, :].bitcast(I32), w1_scales[0, 4 * q : 4 * q + 4, :].bitcast(I32)
-            )
+
+        def load_scales(queue, q):
+            queue.dma_start(w_scales[32 * q : 32 * q + 4, :].bitcast(I32), w1_scales[0, 4 * q : 4 * q + 4, :].bitcast(I32))
+
+        for q in (0, 1):
+            load_scales(nc.sync, q)
         centre = keep.tile([P, V // LANE], U16, name="centre")
         nc.sync.dma_start(centre[:], cen)
-        near = []
-        for d, pos in enumerate((pos1, pos2, pos3, pos4)):
-            lst = keep.tile([P, V // LANE], U16, name=f"near{d}")
-            nc.sync.dma_start(lst[:], pos)
-            near.append(lst)
+        near = [keep.tile([P, V // LANE], U16, name=f"near{d}") for d in range(D)]
+        lists = (pos1, pos2, pos3, pos4)
+        for d in list(range(TURNED, D)) + list(range(TURNED)):
+            nc.sync.dma_start(near[d][:], lists[d])
 
         ident = keep.tile([P, P], F32, name="ident")
         make_identity(nc, ident[:])
-        minus_one = keep.tile([P, V], F32, name="minus_one")
-        nc.gpsimd.memset(minus_one[:], -1.0)
 
         reach_turned = bank(6, V)
         for h in range(HALVES):
             nc.tensor.transpose(reach_turned[:, h * P : (h + 1) * P], reach[:, h * P : (h + 1) * P], ident[:])
         factors = keep.tile([P, HALVES, 2], F32, name="factors")
-        nc.gpsimd.memset(factors[:, :, 0:1], 2.0 / D)
-        for h in range(HALVES):
-            nc.gpsimd.memset(factors[:, h, 1:2], -2.0 * TURNED[h] / D)
+        nc.gpsimd.memset(factors[:, :, 0:1], 2.0)
+        nc.gpsimd.memset(factors[:, :, 1:2], 2.0 / D)
+
+        for q in (2, 3):
+            load_scales(nc.gpsimd, q)
 
         last = PIECES - 1
         grouped = [keep.tile([P, PIECE, PACK], BF16, name=f"grouped{c}", tag=f"grouped{c}", align_bytes=64) for c in range(PIECES)]
@@ -135,6 +135,7 @@ def tile_picked_huber_none_e_kernel(
                 nc.scalar.copy(y[:, cols], acc[:])
 
         halves = [slice(h * P, (h + 1) * P) for h in range(HALVES)]
+        order = list(reversed(range(HALVES)))
         limits = keep.tile([P, V + 2 * HALVES], F32, name="limits", tag="grouped2", align_bytes=64)
         floor = limits[:, 0:V]
         biases = limits[:, V : V + 2 * HALVES].rearrange("p (h u) -> p h u", u=2)
@@ -144,50 +145,41 @@ def tile_picked_huber_none_e_kernel(
         top = keep.tile([P, V], F32, name="top")
         nc.vector.tensor_tensor(top[:], y[:].indirect(centre[:]), reach[:], ALU.add)
         fetched = [keep.tile([P, V], F32, name=f"fetched{d}") for d in range(D)]
-        nc.vector.tensor_tensor(fetched[0][:], y[:].indirect(near[0][:]), minus_one[:], ALU.mult)
-        for d, cols in ((1, halves[1]), (1, halves[0]), (2, halves[0]), (2, halves[1]), (3, slice(0, V))):
-            looked_up = y[:].indirect(entries(near[d], cols.start, cols.stop - cols.start))
-            nc.vector.tensor_tensor(fetched[d][:, cols], looked_up, top[:, cols], ALU.subtract)
+        for d in range(TURNED):
+            nc.scalar.activation(fetched[d][:], y[:].indirect(near[d][:]), COPY, scale=-1.0)
+        for d in range(TURNED, D):
+            nc.vector.tensor_tensor(fetched[d][:], y[:].indirect(near[d][:]), top[:], ALU.subtract)
         totals = [bank(6 + h, P) for h in range(HALVES)]
 
         def turn(target, source, first, final):
             nc.tensor.matmul(target[:], lhsT=source, rhs=ident[:], start=first, stop=final, is_transpose=True)
 
-        first_room = {h: bank(h, P) for h in reversed(range(HALVES))}
-        for h in first_room:
-            turn(first_room[h], top[:, halves[h]], True, False)
-        for h in first_room:
-            turned = bank(4 + h, P)
-            turn(turned, top[:, halves[h]], True, True)
-            base = keep.tile([P, P], F32, name=f"base{h}")
-            nc.scalar.activation(base[:], turned[:], IDENTITY, bias=biases[:, h, 1:2])
-            turn(totals[h], base[:], True, False)
-        for d in range(max(TURNED)):
-            turned_halves = sorted((h for h in range(HALVES) if d < TURNED[h]), key=lambda h: TURNED[h])
-            room = first_room if d == 0 else {h: bank(HALVES * d + h, P) for h in turned_halves}
-            short = {}
-            for h in turned_halves:
-                turn(room[h], fetched[d][:, halves[h]], d > 0, True)
-                short[h] = keep.tile([P, P], F32, name=f"under{d}_{h}")
-                nc.scalar.activation(short[h][:], room[h][:], RELU, scale=1.0 if d == 0 else -1.0)
-            for h in turned_halves:
-                pull = keep.tile([P, P], F32, name=f"pull{d}_{h}")
-                nc.scalar.activation(pull[:], short[h][:], RELU, bias=biases[:, h, 0:1], scale=-1.0 / D)
-                turn(totals[h], pull[:], False, d == TURNED[h] - 1)
+        room = {(d, h): bank(HALVES * d + h, P) for d in range(TURNED) for h in order}
+        for d, h in room:
+            opening, closing = (top, fetched[d]) if d == 0 else (fetched[d], top)
+            turn(room[d, h], opening[:, halves[h]], True, False)
+            turn(room[d, h], closing[:, halves[h]], False, True)
+        for d in range(TURNED):
+            above = {}
+            for h in order:
+                above[h] = keep.tile([P, P], F32, name=f"above{d}_{h}")
+                nc.scalar.activation(above[h][:], room[d, h][:], RELU, bias=biases[:, h, 0:1], scale=-1.0)
+            for h in order:
+                lack = keep.tile([P, P], F32, name=f"lack{d}_{h}")
+                nc.scalar.activation(lack[:], above[h][:], RELU, bias=biases[:, h, 1:2], scale=-1.0 / D)
+                turn(totals[h], lack[:], d == 0, d == TURNED - 1)
 
-        def clip(d, h):
-            clipped = keep.tile([P, P], F32, name=f"clipped{d}_{h}")
-            nc.vector.scalar_tensor_tensor(clipped[:], fetched[d][:, halves[h]], 0.0, floor[:, halves[h]], ALU.min, ALU.max)
-            return clipped
-
-        def add_share(name, clipped, rest):
-            res = keep.tile([P, P], F32, name=name)
-            nc.vector.scalar_tensor_tensor(res[:], clipped[:], 1.0 / D, rest[:], ALU.mult, ALU.add)
-            return res
-
-        third_1 = clip(2, 1)
-        fourth_1 = clip(3, 1)
-        partial_1 = add_share("partial_1", third_1, totals[1])
-        fourth_0 = clip(3, 0)
-        nc.sync.dma_start(out[:, halves[1]], add_share("res1", fourth_1, partial_1)[:])
-        nc.sync.dma_start(out[:, halves[0]], add_share("res0", fourth_0, totals[0])[:])
+        clipped = {}
+        for d in range(TURNED, D):
+            clipped[d] = keep.tile([P, V], F32, name=f"clipped{d}")
+            nc.vector.scalar_tensor_tensor(clipped[d][:], fetched[d][:], 0.0, floor, ALU.min, ALU.max)
+        running = {h: top[:, halves[h]] for h in order}
+        for d in range(TURNED, D):
+            for h in order:
+                summed = keep.tile([P, P], F32, name=f"summed{d}_{h}")
+                nc.vector.scalar_tensor_tensor(summed[:], clipped[d][:, halves[h]], 1.0 / D, running[h], ALU.mult, ALU.add)
+                running[h] = summed[:]
+        for h in order:
+            res = keep.tile([P, P], F32, name=f"res{h}")
+            nc.vector.tensor_tensor(res[:], running[h], totals[h][:], ALU.subtract)
+            nc.sync.dma_start(out[:, halves[h]], res[:])

@@ -60,13 +60,12 @@ def tile_picked_huber_none_e_kernel(
         def load_scales(queue, q):
             queue.dma_start(w_scales[32 * q : 32 * q + 4, :].bitcast(I32), w1_scales[0, 4 * q : 4 * q + 4, :].bitcast(I32))
 
-        for q in (0, 1):
-            load_scales(nc.sync, q)
+        load_scales(nc.sync, 0)
         centre = keep.tile([P, V // LANE], U16, name="centre")
         nc.sync.dma_start(centre[:], cen)
         near = [keep.tile([P, V // LANE], U16, name=f"near{d}") for d in range(D)]
         lists = (pos1, pos2, pos3, pos4)
-        for d in list(range(TURNED, D)) + list(range(TURNED)):
+        for d in range(D):
             nc.sync.dma_start(near[d][:], lists[d])
 
         ident = keep.tile([P, P], F32, name="ident")
@@ -79,7 +78,7 @@ def tile_picked_huber_none_e_kernel(
         nc.gpsimd.memset(factors[:, :, 0:1], 2.0)
         nc.gpsimd.memset(factors[:, :, 1:2], 2.0 / D)
 
-        for q in (2, 3):
+        for q in (1, 2, 3):
             load_scales(nc.gpsimd, q)
 
         last = PIECES - 1
@@ -142,31 +141,34 @@ def tile_picked_huber_none_e_kernel(
         nc.vector.tensor_scalar(floor, reach[:], -2.0, None, ALU.mult)
         nc.vector.tensor_tensor(biases, reach_turned[:].rearrange("p (h m) -> p h m", m=P)[:, :, 0:2], factors[:], ALU.mult)
 
+        def looked_up(offsets, cols):
+            return y[:].indirect(entries(offsets, cols.start, cols.stop - cols.start))
+
         top = keep.tile([P, V], F32, name="top")
-        nc.vector.tensor_tensor(top[:], y[:].indirect(centre[:]), reach[:], ALU.add)
         fetched = [keep.tile([P, V], F32, name=f"fetched{d}") for d in range(D)]
-        for d in range(TURNED):
-            nc.scalar.activation(fetched[d][:], y[:].indirect(near[d][:]), COPY, scale=-1.0)
-        for d in range(TURNED, D):
-            nc.vector.tensor_tensor(fetched[d][:], y[:].indirect(near[d][:]), top[:], ALU.subtract)
+        for h in order:
+            nc.vector.tensor_tensor(top[:, halves[h]], looked_up(centre, halves[h]), reach[:, halves[h]], ALU.add)
+        for h in order:
+            for d in range(TURNED):
+                nc.scalar.activation(fetched[d][:, halves[h]], looked_up(near[d], halves[h]), COPY, scale=-1.0)
+        for d, cols in ((2, halves[1]), (2, halves[0]), (3, slice(0, V))):
+            nc.vector.tensor_tensor(fetched[d][:, cols], looked_up(near[d], cols), top[:, cols], ALU.subtract)
         totals = [bank(6 + h, P) for h in range(HALVES)]
 
         def turn(target, source, first, final):
             nc.tensor.matmul(target[:], lhsT=source, rhs=ident[:], start=first, stop=final, is_transpose=True)
 
-        room = {(d, h): bank(HALVES * d + h, P) for d in range(TURNED) for h in order}
-        for d, h in room:
-            opening, closing = (top, fetched[d]) if d == 0 else (fetched[d], top)
-            turn(room[d, h], opening[:, halves[h]], True, False)
-            turn(room[d, h], closing[:, halves[h]], False, True)
-        for d in range(TURNED):
-            above = {}
-            for h in order:
-                above[h] = keep.tile([P, P], F32, name=f"above{d}_{h}")
-                nc.scalar.activation(above[h][:], room[d, h][:], RELU, bias=biases[:, h, 0:1], scale=-1.0)
-            for h in order:
+        room = {(h, d): bank(HALVES * d + h, P) for h in order for d in range(TURNED)}
+        for h, d in room:
+            turn(room[h, d], top[:, halves[h]], True, False)
+            turn(room[h, d], fetched[d][:, halves[h]], False, True)
+        for h in order:
+            above = [keep.tile([P, P], F32, name=f"above{d}_{h}") for d in range(TURNED)]
+            for d in range(TURNED):
+                nc.scalar.activation(above[d][:], room[h, d][:], RELU, bias=biases[:, h, 0:1], scale=-1.0)
+            for d in range(TURNED):
                 lack = keep.tile([P, P], F32, name=f"lack{d}_{h}")
-                nc.scalar.activation(lack[:], above[h][:], RELU, bias=biases[:, h, 1:2], scale=-1.0 / D)
+                nc.scalar.activation(lack[:], above[d][:], RELU, bias=biases[:, h, 1:2], scale=-1.0 / D)
                 turn(totals[h], lack[:], d == 0, d == TURNED - 1)
 
         clipped = {}

@@ -25,8 +25,7 @@ PIECES = S // PIECE
 HALVES = V // P
 LANE = 16
 TURNED = 2
-CAST_SPLIT = 704
-LOAD_ORDER = (0, 2, 1, 3)
+LAY_BEFORE = {0: (PIECE, PIECE), 1: (2 * PIECE, PIECE)}
 
 
 def entries(offsets, first, count):
@@ -48,9 +47,9 @@ def tile_picked_huber_none_e_kernel(
         rows = xT.rearrange("(p j) t -> j p t", j=PACK)
         planes = [keep.tile([P, T], F32, name=f"plane{j}") for j in range(PACK)]
         picked = keep.tile([P, S // LANE], U16, name="picked")
-        nc.sync.dma_start(planes[LOAD_ORDER[0]][:], rows[LOAD_ORDER[0]])
+        nc.sync.dma_start(planes[0][:], rows[0])
         nc.sync.dma_start(picked[:], offs)
-        for j in LOAD_ORDER[1:]:
+        for j in range(1, PACK):
             nc.sync.dma_start(planes[j][:], rows[j])
         reach = keep.tile([P, V], F32, name="reach")
         nc.sync.dma_start(reach[:], bound)
@@ -76,58 +75,48 @@ def tile_picked_huber_none_e_kernel(
             nc.tensor.transpose(reach_turned[:, h * P : (h + 1) * P], reach[:, h * P : (h + 1) * P], ident[:])
         factors = keep.tile([P, HALVES, 2], F32, name="factors")
         nc.gpsimd.memset(factors[:, :, 0:1], 2.0)
-        nc.gpsimd.memset(factors[:, :, 1:2], 2.0 / D)
+        nc.scalar.activation(factors[:, :, 1:2], factors[:, :, 0:1], COPY, scale=1.0 / D)
 
         for q in (1, 2, 3):
             load_scales(nc.gpsimd, q)
 
-        last = PIECES - 1
-        grouped = [keep.tile([P, PIECE, PACK], BF16, name=f"grouped{c}", tag=f"grouped{c}", align_bytes=64) for c in range(PIECES)]
-        paired = keep.tile([P, last, 2, PIECE, 2], BF16, name="paired")
-        pairs = [paired[:, c] for c in range(last)]
+        grouped = keep.tile([P, S, PACK], BF16, name="grouped", tag="grouped", align_bytes=64)
+        flat = keep.tile([P, PACK, S - PIECE], BF16, name="flat")
 
-        def slots(j):
-            cuts = ((0, last),) if j == 2 else ((0, 2), (2, last))
-            return [(paired[:, a:b, j // 2, :, j % 2], entries(picked, a * PIECE, (b - a) * PIECE)) for a, b in cuts] + [
-                (grouped[last][:, :, j], entries(picked, last * PIECE, PIECE)),
-            ]
+        def lay(engine_copy, word, first, count):
+            slots = slice(2 * word, 2 * word + 2)
+            source = flat[:, slots, first - PIECE : first - PIECE + count].rearrange("p j s -> p s j")
+            engine_copy(grouped[:, first : first + count, slots], source)
 
-        for j in LOAD_ORDER:
-            if j >= 2:
-                for target, offsets in slots(j):
-                    nc.vector.tensor_copy(target, planes[j][:].indirect(offsets))
-                continue
-            rounded = keep.tile([P, T], BF16, name=f"rounded{j}")
-            if j == 0:
-                nc.scalar.copy(rounded[:], planes[j][:])
-            else:
-                nc.scalar.copy(rounded[:, 0:CAST_SPLIT], planes[j][:, 0:CAST_SPLIT])
-                nc.vector.tensor_copy(rounded[:, CAST_SPLIT:T], planes[j][:, CAST_SPLIT:T])
-            (target, offsets), *rest = slots(j)
-            nc.vector.tensor_copy(target, planes[j][:].indirect(offsets))
-            for target, offsets in rest:
-                nc.scalar.activation(target, rounded[:].indirect(offsets), COPY)
-        runs = [(0, 0, PIECE), (1, 0, PIECE), (last, 0, PIECE), (2, 0, PIECE // 2), (2, PIECE // 2, PIECE // 2)]
-        for c, first, count in runs:
-            if c != last:
-                words = grouped[c][:].rearrange("p s j -> p (s j)").bitcast(U32).rearrange("p (s u) -> p s u", u=2)
-                halves_of = pairs[c].rearrange("p u s e -> p u (s e)").bitcast(U32).rearrange("p u s -> p s u")
-                nc.scalar.copy(words[:, first : first + count], halves_of[:, first : first + count])
+        runs = [(0, PIECE), (PIECE, PIECE), (2 * PIECE, PIECE), (3 * PIECE, PIECE // 2), (3 * PIECE + PIECE // 2, PIECE // 2)]
+        for j in range(PACK):
+            nc.vector.tensor_copy(grouped[:, 0:PIECE, j], planes[j][:].indirect(entries(picked, 0, PIECE)))
+            cuts = [(PIECE, S - PIECE)] if j < PACK - 1 else runs[1:]
+            for first, count in cuts:
+                target = flat[:, j, first - PIECE : first - PIECE + count]
+                nc.scalar.activation(target, planes[j][:].indirect(entries(picked, first, count)), COPY)
+            if j == 1:
+                lay(nc.vector.tensor_copy, 0, PIECE, S - PIECE)
+        for first, count in runs:
+            if first >= 3 * PIECE:
+                lay(nc.scalar.copy, 1, first, count)
 
         y = keep.tile([P, S], F32, name="y")
-        for i, (c, first, count) in enumerate(runs):
-            codes = keep.tile([P, count], U32, name=f"codes{i}", tag="grouped0" if c == last else f"codes{i}", align_bytes=64)
+        for i, (first, count) in enumerate(runs):
+            if i in LAY_BEFORE:
+                lay(nc.vector.tensor_copy, 1, *LAY_BEFORE[i])
+            codes = keep.tile([P, count], U32, name=f"codes{i}", align_bytes=64)
             scales = keep.tile([P, count], U8, name=f"scales{i}", align_bytes=64)
             nc.vector.quantize_mx(
                 out=codes[:].bitcast(FP8X4), scales=scales[:],
-                in_=grouped[c][:, first : first + count].rearrange("p s j -> p (s j)"),
+                in_=grouped[:, first : first + count].rearrange("p s j -> p (s j)"),
             )
             acc = bank(i, count)
             nc.tensor.matmul_mx(
                 out=acc[:], lhsT=w_codes[:].bitcast(FP8X4), lhsT_scale=w_scales[:],
                 rhs=codes[:].bitcast(FP8X4), rhs_scale=scales[:], start=True, stop=True,
             )
-            cols = slice(c * PIECE + first, c * PIECE + first + count)
+            cols = slice(first, first + count)
             if i % 2 == 1:
                 nc.vector.tensor_copy(y[:, cols], acc[:])
             else:
@@ -135,7 +124,7 @@ def tile_picked_huber_none_e_kernel(
 
         halves = [slice(h * P, (h + 1) * P) for h in range(HALVES)]
         order = list(reversed(range(HALVES)))
-        limits = keep.tile([P, V + 2 * HALVES], F32, name="limits", tag="grouped2", align_bytes=64)
+        limits = keep.tile([P, V + 2 * HALVES], F32, name="limits", tag="grouped", align_bytes=64)
         floor = limits[:, 0:V]
         biases = limits[:, V : V + 2 * HALVES].rearrange("p (h u) -> p h u", u=2)
         nc.vector.tensor_scalar(floor, reach[:], -2.0, None, ALU.mult)

@@ -151,14 +151,25 @@ def tile_picked_huber_none_e_kernel(
         for h, d in room:
             turn(room[h, d], top[:, halves[h]], True, False)
             turn(room[h, d], fetched[d][:, halves[h]], False, True)
-        for h in order:
-            above = [keep.tile([P, P], F32, name=f"above{d}_{h}") for d in range(TURNED)]
-            for d in range(TURNED):
-                nc.scalar.activation(above[d][:], room[h, d][:], RELU, bias=biases[:, h, 0:1], scale=-1.0)
-            for d in range(TURNED):
-                lack = keep.tile([P, P], F32, name=f"lack{d}_{h}")
-                nc.scalar.activation(lack[:], above[d][:], RELU, bias=biases[:, h, 1:2], scale=-1.0 / D)
-                turn(totals[h], lack[:], d == 0, d == TURNED - 1)
+        blocks = list(room)
+        above = {b: keep.tile([P, P], F32, name=f"above{b[1]}_{b[0]}") for b in blocks}
+
+        def first_relu(h, d):
+            nc.scalar.activation(above[h, d][:], room[h, d][:], RELU, bias=biases[:, h, 0:1], scale=-1.0)
+
+        def second_relu(h, d, lack):
+            nc.scalar.activation(lack, above[h, d][:], RELU, bias=biases[:, h, 1:2], scale=-1.0 / D)
+            turn(totals[h], lack, d == 0, d == TURNED - 1)
+
+        first_relu(*blocks[0])
+        for i, block in enumerate(blocks):
+            if i + 1 < len(blocks):
+                first_relu(*blocks[i + 1])
+            if i == 1:
+                h, d = blocks[i + 1]
+                second_relu(*block, fetched[d][:, halves[h]])
+            else:
+                second_relu(*block, keep.tile([P, P], F32, name=f"lack{i}")[:])
 
         clipped = {}
         for d in range(TURNED, D):

from contextlib import ExitStack

import concourse.mybir as mybir
from concourse.masks import make_identity

K, T, S, V, N = 512, 1024, 512, 256, 128
D = 4
FLOPS = 2 * K * N * S

F32 = mybir.dt.float32
BF16 = mybir.dt.bfloat16
I32 = mybir.dt.int32
U32 = mybir.dt.uint32
U16 = mybir.dt.uint16
U8 = mybir.dt.uint8
FP8X4 = mybir.dt.float8_e4m3fn_x4
ALU = mybir.AluOpType
COPY = mybir.ActivationFunctionType.Copy
RELU = mybir.ActivationFunctionType.Relu

P = 128
PACK = 4
PIECE = 128
PIECES = S // PIECE
HALVES = V // P
LANE = 16
TURNED = 2
LAY_BEFORE = {0: (PIECE, PIECE), 1: (2 * PIECE, PIECE)}


def entries(offsets, first, count):
    return offsets[:, first // LANE : (first + count) // LANE]


def tile_picked_huber_none_e_kernel(
    tc, xT, w1_words, w1_scales, bound, offs, cen, pos1, pos2, pos3, pos4, out
):
    nc = tc.nc
    with ExitStack() as ctx:
        keep = ctx.enter_context(tc.tile_pool(name="keep", bufs=1))
        psum = ctx.enter_context(tc.psum_pool(name="psum", bufs=1))

        def bank(i, width):
            return psum.tile([P, width], F32, name=f"bank{i}", tag=f"bank{i}")

        w_scales = keep.tile([P, N], U8, name="w_scales", align_bytes=64)
        rows = xT.rearrange("(p j) t -> j p t", j=PACK)
        planes = [keep.tile([P, T], F32, name=f"plane{j}") for j in range(PACK)]
        picked = keep.tile([P, S // LANE], U16, name="picked")
        nc.sync.dma_start(planes[0][:], rows[0])
        nc.sync.dma_start(picked[:], offs)
        for j in range(1, PACK):
            nc.sync.dma_start(planes[j][:], rows[j])
        reach = keep.tile([P, V], F32, name="reach")
        nc.sync.dma_start(reach[:], bound)
        w_codes = keep.tile([P, N], U32, name="w_codes", align_bytes=64)
        nc.sync.dma_start(w_codes[:].bitcast(I32), w1_words[0].rearrange("p n t -> p (n t)").bitcast(I32))

        def load_scales(queue, q):
            queue.dma_start(w_scales[32 * q : 32 * q + 4, :].bitcast(I32), w1_scales[0, 4 * q : 4 * q + 4, :].bitcast(I32))

        load_scales(nc.sync, 0)
        centre = keep.tile([P, V // LANE], U16, name="centre")
        nc.sync.dma_start(centre[:], cen)
        near = [keep.tile([P, V // LANE], U16, name=f"near{d}") for d in range(D)]
        lists = (pos1, pos2, pos3, pos4)
        for d in range(D):
            nc.sync.dma_start(near[d][:], lists[d])

        ident = keep.tile([P, P], F32, name="ident")
        make_identity(nc, ident[:])

        reach_turned = bank(6, V)
        for h in range(HALVES):
            nc.tensor.transpose(reach_turned[:, h * P : (h + 1) * P], reach[:, h * P : (h + 1) * P], ident[:])
        factors = keep.tile([P, HALVES, 2], F32, name="factors")
        nc.gpsimd.memset(factors[:, :, 0:1], 2.0)
        nc.scalar.activation(factors[:, :, 1:2], factors[:, :, 0:1], COPY, scale=1.0 / D)

        for q in (1, 2, 3):
            load_scales(nc.gpsimd, q)

        grouped = keep.tile([P, S, PACK], BF16, name="grouped", tag="grouped", align_bytes=64)
        flat = keep.tile([P, PACK, S - PIECE], BF16, name="flat")

        def lay(engine_copy, word, first, count):
            slots = slice(2 * word, 2 * word + 2)
            source = flat[:, slots, first - PIECE : first - PIECE + count].rearrange("p j s -> p s j")
            engine_copy(grouped[:, first : first + count, slots], source)

        runs = [(0, PIECE), (PIECE, PIECE), (2 * PIECE, PIECE), (3 * PIECE, PIECE // 2), (3 * PIECE + PIECE // 2, PIECE // 2)]
        for j in range(PACK):
            nc.vector.tensor_copy(grouped[:, 0:PIECE, j], planes[j][:].indirect(entries(picked, 0, PIECE)))
            cuts = [(PIECE, S - PIECE)] if j < PACK - 1 else runs[1:]
            for first, count in cuts:
                target = flat[:, j, first - PIECE : first - PIECE + count]
                nc.scalar.activation(target, planes[j][:].indirect(entries(picked, first, count)), COPY)
            if j == 1:
                lay(nc.vector.tensor_copy, 0, PIECE, S - PIECE)
        for first, count in runs:
            if first >= 3 * PIECE:
                lay(nc.scalar.copy, 1, first, count)

        y = keep.tile([P, S], F32, name="y")
        for i, (first, count) in enumerate(runs):
            if i in LAY_BEFORE:
                lay(nc.vector.tensor_copy, 1, *LAY_BEFORE[i])
            codes = keep.tile([P, count], U32, name=f"codes{i}", align_bytes=64)
            scales = keep.tile([P, count], U8, name=f"scales{i}", align_bytes=64)
            nc.vector.quantize_mx(
                out=codes[:].bitcast(FP8X4), scales=scales[:],
                in_=grouped[:, first : first + count].rearrange("p s j -> p (s j)"),
            )
            acc = bank(i, count)
            nc.tensor.matmul_mx(
                out=acc[:], lhsT=w_codes[:].bitcast(FP8X4), lhsT_scale=w_scales[:],
                rhs=codes[:].bitcast(FP8X4), rhs_scale=scales[:], start=True, stop=True,
            )
            cols = slice(first, first + count)
            if i % 2 == 1:
                nc.vector.tensor_copy(y[:, cols], acc[:])
            else:
                nc.scalar.copy(y[:, cols], acc[:])

        halves = [slice(h * P, (h + 1) * P) for h in range(HALVES)]
        order = list(reversed(range(HALVES)))
        limits = keep.tile([P, V + 2 * HALVES], F32, name="limits", tag="grouped", align_bytes=64)
        floor = limits[:, 0:V]
        biases = limits[:, V : V + 2 * HALVES].rearrange("p (h u) -> p h u", u=2)
        nc.vector.tensor_scalar(floor, reach[:], -2.0, None, ALU.mult)
        nc.vector.tensor_tensor(biases, reach_turned[:].rearrange("p (h m) -> p h m", m=P)[:, :, 0:2], factors[:], ALU.mult)

        def looked_up(offsets, cols):
            return y[:].indirect(entries(offsets, cols.start, cols.stop - cols.start))

        top = keep.tile([P, V], F32, name="top")
        fetched = [keep.tile([P, V], F32, name=f"fetched{d}") for d in range(D)]
        for h in order:
            nc.vector.tensor_tensor(top[:, halves[h]], looked_up(centre, halves[h]), reach[:, halves[h]], ALU.add)
        for h in order:
            for d in range(TURNED):
                nc.scalar.activation(fetched[d][:, halves[h]], looked_up(near[d], halves[h]), COPY, scale=-1.0)
        for d, cols in ((2, halves[1]), (2, halves[0]), (3, slice(0, V))):
            nc.vector.tensor_tensor(fetched[d][:, cols], looked_up(near[d], cols), top[:, cols], ALU.subtract)
        totals = [bank(6 + h, P) for h in range(HALVES)]

        def turn(target, source, first, final):
            nc.tensor.matmul(target[:], lhsT=source, rhs=ident[:], start=first, stop=final, is_transpose=True)

        room = {(h, d): bank(HALVES * d + h, P) for h in order for d in range(TURNED)}
        for h, d in room:
            turn(room[h, d], top[:, halves[h]], True, False)
            turn(room[h, d], fetched[d][:, halves[h]], False, True)
        blocks = list(room)
        above = {b: keep.tile([P, P], F32, name=f"above{b[1]}_{b[0]}") for b in blocks}

        def first_relu(h, d):
            nc.scalar.activation(above[h, d][:], room[h, d][:], RELU, bias=biases[:, h, 0:1], scale=-1.0)

        def second_relu(h, d, lack):
            nc.scalar.activation(lack, above[h, d][:], RELU, bias=biases[:, h, 1:2], scale=-1.0 / D)
            turn(totals[h], lack, d == 0, d == TURNED - 1)

        first_relu(*blocks[0])
        for i, block in enumerate(blocks):
            if i + 1 < len(blocks):
                first_relu(*blocks[i + 1])
            if i == 1:
                h, d = blocks[i + 1]
                second_relu(*block, fetched[d][:, halves[h]])
            else:
                second_relu(*block, keep.tile([P, P], F32, name=f"lack{i}")[:])

        clipped = {}
        for d in range(TURNED, D):
            clipped[d] = keep.tile([P, V], F32, name=f"clipped{d}")
            nc.vector.scalar_tensor_tensor(clipped[d][:], fetched[d][:], 0.0, floor, ALU.min, ALU.max)
        running = {h: top[:, halves[h]] for h in order}
        for d in range(TURNED, D):
            for h in order:
                summed = keep.tile([P, P], F32, name=f"summed{d}_{h}")
                nc.vector.scalar_tensor_tensor(summed[:], clipped[d][:, halves[h]], 1.0 / D, running[h], ALU.mult, ALU.add)
                running[h] = summed[:]
        for h in order:
            res = keep.tile([P, P], F32, name=f"res{h}")
            nc.vector.tensor_tensor(res[:], running[h], totals[h][:], ALU.subtract)
            nc.sync.dma_start(out[:, halves[h]], res[:])
